import numpy as np
import ml_dtypes


def mxq(x, axis, fmt="e4m3"):
    dtype, down = {"e4m3": (ml_dtypes.float8_e4m3fn, 7), "e5m2": (ml_dtypes.float8_e5m2, 14)}[fmt]
    v = np.moveaxis(np.asarray(x, np.float32).astype(ml_dtypes.bfloat16).astype(np.float64), axis, -1)
    blocks = v.reshape(v.shape[:-1] + (-1, 32))
    amax = np.abs(blocks).max(-1, keepdims=True)
    byte = np.maximum(np.where(amax > 0, np.frexp(amax)[1] - 1 + 127, 0) - down, 1)
    scale = np.exp2(byte - 127.0)
    codes = (blocks / scale).astype(np.float32).astype(dtype).astype(np.float64)
    return np.moveaxis((codes * scale).reshape(v.shape), -1, axis)


WIDE = False


def mx_kscale(k):
    if not WIDE:
        return np.ones(k)
    levels = np.array([10, -10, 5, -5, 0])
    if k % 512:
        return np.exp2(np.random.permutation(np.resize(levels, k // 32))).repeat(32)
    a = np.empty((k // 512, 16))
    for p in range(k // 512):
        a[p, :8] = np.random.permutation(np.resize(levels, 8))
        for g in range(8):
            far = levels[np.abs(levels - a[p, g]) >= 10]
            a[p, g + 8] = far[np.random.randint(len(far))]
    return np.exp2(a.ravel()).repeat(32)


def f64(x):
    return np.asarray(x).astype(np.float64)


def striped(idx):
    return np.tile(idx.reshape(-1, 16).T, (8, 1)).astype(np.uint16)


def unstriped(offs):
    return offs[:16].T.reshape(-1).astype(np.int64)


def pack_weight(w):
    k, n = w.shape
    w = f64(np.asarray(w, np.float32).astype(ml_dtypes.bfloat16)).reshape(k // 32, 32, n)
    amax = np.abs(w).max(1)
    byte = np.clip(np.where(amax > 0, np.frexp(amax)[1] - 1 + 127 - 7, 1), 1, 254)
    scaled = (w * np.exp2(127.0 - byte)[:, None, :]).reshape(k, n).astype(np.float32)
    words = np.ascontiguousarray(scaled.reshape(k // 512, 128, 4, n).transpose(0, 1, 3, 2)).astype(ml_dtypes.float8_e4m3fn).view(np.uint8)
    return words, np.ascontiguousarray(byte.astype(np.uint8).reshape(k // 512, 16, n))


def unpack_weight(words, scales):
    g, p, n, _ = words.shape
    vals = np.ascontiguousarray(words).view(ml_dtypes.float8_e4m3fn).astype(np.float64) * np.repeat(np.exp2(scales.astype(np.float64) - 127.0), 8, axis=1)[..., None]
    return vals.transpose(0, 1, 3, 2).reshape(g * 512, n)


def sigmoid(v):
    return 1.0 / (1.0 + np.exp(-np.maximum(v, -700.0)))


K, T, S, H, D, V, W, U = 512, 1024, 512, 512, 2, 256, 1024, 512
P = 2 ** 7


def setup_inputs():
    n = np.random.standard_normal
    s = mx_kscale(K)[:, None]
    u = mx_kscale(H)
    packed_xT = pack_weight(n((K, T)) * s)
    packed_eT = pack_weight(n((H, W)) / np.sqrt(H) / u[:, None])
    return {
        "x_words": packed_xT[0],
        "x_scales": packed_xT[1],
        "w1": (n((K, H)) / np.sqrt(K) / s * u).astype(np.float32),
        "e_words": packed_eT[0],
        "e_scales": packed_eT[1],
        "gain": (np.tile(np.random.uniform(0.5, 1.0, V), (P, 1))).astype(np.float32),
        "offs": striped(np.random.permutation(T)[:S]),
        "pos": striped(np.random.permutation(W)[:V]),
        "neg": striped(np.random.permutation(W)[:U]),
    }


def reference(x_words, x_scales, w1, e_words, e_scales, gain, offs, pos, neg):
    xq = unpack_weight(x_words, x_scales)[:, unstriped(offs)]
    h = mxq(f64(w1), 0, "e4m3").T @ xq
    hq = mxq(h, 0, "e4m3")
    e_neg = unpack_weight(e_words, e_scales)[:, unstriped(neg)]
    z = hq.T @ e_neg
    e_pos = unpack_weight(e_words, e_scales)[:, unstriped(pos)]
    y = hq.T @ e_pos
    gg = sigmoid(4.0 * (z - np.repeat(y, D, axis=1)))
    rr = gg.reshape(len(gg), -1, D).sum(axis=2)
    return np.log(rr + 1.0) * f64(gain)[:1]

@@ -1,0 +1,128 @@
+from contextlib import ExitStack
+
+import concourse.mybir as mybir
+
+F32 = mybir.dt.float32
+BF16 = mybir.dt.bfloat16
+I32 = mybir.dt.int32
+U32 = mybir.dt.uint32
+U16 = mybir.dt.uint16
+U8 = mybir.dt.uint8
+FP8X4 = mybir.dt.float8_e4m3fn_x4
+ACT = mybir.ActivationFunctionType
+ALU = mybir.AluOpType
+
+P = 128
+K, T, S, H, D, V, W, U = 512, 1024, 512, 512, 2, 256, 1024, 512
+TILES = S // P
+FLOPS = 2 * K * H * S + 2 * H * S * U + 2 * H * S * V
+
+
+def tile_picked_ysmap_log_p_kernel(
+    tc, x_words, x_scales, w1, e_words, e_scales, gain, offs, pos, neg, out
+):
+    nc = tc.nc
+    with ExitStack() as ctx:
+        keep = ctx.enter_context(tc.tile_pool(name="keep", bufs=1))
+        psum = ctx.enter_context(tc.psum_pool(name="psum", bufs=1))
+
+        offs_sb = keep.tile([P, S // 16], U16, name="offs_sb")
+        neg_sb = keep.tile([P, U // 16], U16, name="neg_sb")
+        pos_sb = keep.tile([P, V // 16], U16, name="pos_sb")
+        xs_all = keep.tile([P, T], U8, name="xs_all", align_bytes=64)
+        es_all = keep.tile([P, W], U8, name="es_all", align_bytes=64)
+        xw_all = keep.tile([P, T], I32, name="xw_all", align_bytes=64)
+        ew_all = keep.tile([P, W], I32, name="ew_all", align_bytes=64)
+        w_raw = [keep.tile([P, 4, H // 2], F32, name=f"w_raw{a}", align_bytes=64) for a in range(2)]
+        gain_sb = keep.tile([P, V], F32, name="gain_sb")
+
+        nc.vector.memset(xs_all[:].bitcast(I32), 0)
+        nc.vector.memset(es_all[:].bitcast(I32), 0)
+
+        w_view = w1.rearrange("(p j) c -> p j c", j=4)
+        nc.sync.dma_start(offs_sb[:], offs)
+        for q in range(4):
+            nc.scalar.dma_start(xs_all[32 * q : 32 * q + 4, :].bitcast(I32), x_scales[0, 4 * q : 4 * q + 4, :].bitcast(I32))
+        nc.sync.dma_start(neg_sb[:], neg)
+        nc.sync.dma_start(pos_sb[:], pos)
+        nc.sync.dma_start(w_raw[0][:], w_view[:, :, 0 : H // 2])
+        for q in range(4):
+            nc.scalar.dma_start(es_all[32 * q : 32 * q + 4, :].bitcast(I32), e_scales[0, 4 * q : 4 * q + 4, :].bitcast(I32))
+        nc.sync.dma_start(w_raw[1][:], w_view[:, :, H // 2 : H])
+        nc.sync.dma_start(xw_all[:], x_words[0].rearrange("p n t -> p (n t)").bitcast(I32))
+        nc.sync.dma_start(ew_all[:], e_words[0].rearrange("p n t -> p (n t)").bitcast(I32))
+        nc.sync.dma_start(gain_sb[:], gain)
+
+        xs = keep.tile([P, S], U8, name="xs", align_bytes=64)
+        ns = keep.tile([P, U], U8, name="ns", align_bytes=64)
+        ps = keep.tile([P, V], U8, name="ps", align_bytes=64)
+        xw = [keep.tile([P, P], U32, name=f"xw{i}", align_bytes=64) for i in range(TILES)]
+        nw = keep.tile([P, U], U32, name="nw", align_bytes=64)
+        pw = keep.tile([P, V], U32, name="pw", align_bytes=64)
+
+        nc.vector.tensor_copy(xs[:], xs_all[:].indirect(offs_sb[:]))
+        nc.vector.tensor_copy(ns[:], es_all[:].indirect(neg_sb[:]))
+        nc.vector.tensor_copy(ps[:], es_all[:].indirect(pos_sb[:]))
+
+        w_bf = keep.tile([P, 4, P, 4], BF16, name="w_bf", align_bytes=64)
+        for a in range(2):
+            nc.scalar.activation(
+                w_bf[:, :, 64 * a : 64 * a + 64, :].rearrange("p t m j -> p m t j"),
+                w_raw[a][:].rearrange("p j (m t) -> p m t j", t=4),
+                ACT.Copy,
+            )
+        wq = keep.tile([P, H], U32, name="wq", align_bytes=64)
+        wq_s = keep.tile([P, H], U8, name="wq_s", align_bytes=64)
+        nc.vector.quantize_mx(out=wq[:].bitcast(FP8X4), scales=wq_s[:], in_=w_bf[:].rearrange("p t m j -> p (t m j)"))
+
+        for i in range(TILES):
+            nc.vector.tensor_copy(xw[i][:], xw_all[:].bitcast(U32).indirect(offs_sb[:, 8 * i : 8 * i + 8]))
+
+        h_bf = []
+        for i in range(TILES):
+            h_ps = psum.tile([P, 4, P], F32, name="h_ps", bufs=3)
+            for t in range(4):
+                nc.tensor.matmul_mx(
+                    out=h_ps[:, t, :],
+                    lhsT=wq[:, P * t : P * (t + 1)].bitcast(FP8X4),
+                    lhsT_scale=wq_s[:, P * t : P * (t + 1)],
+                    rhs=xw[i][:].bitcast(FP8X4),
+                    rhs_scale=xs[:, P * i : P * (i + 1)],
+                    start=True,
+                    stop=True,
+                )
+            hb = keep.tile([P, P, 4], BF16, name=f"h_bf{i}", align_bytes=64)
+            nc.scalar.activation(hb[:], h_ps[:].rearrange("p t n -> p n t"), ACT.Copy)
+            h_bf.append(hb)
+
+        nc.vector.tensor_copy(nw[:], ew_all[:].bitcast(U32).indirect(neg_sb[:]))
+        nc.vector.tensor_copy(pw[:], ew_all[:].bitcast(U32).indirect(pos_sb[:]))
+
+        sums = []
+        for i in range(TILES):
+            hq = keep.tile([P, P], U32, name=f"hq{i}", align_bytes=64)
+            hq_s = keep.tile([P, P], U8, name=f"hq_s{i}", align_bytes=64)
+            nc.vector.quantize_mx(out=hq[:].bitcast(FP8X4), scales=hq_s[:], in_=h_bf[i][:].rearrange("p n t -> p (n t)"))
+            y_ps = psum.tile([P, V], F32, name="y_ps", bufs=2)
+            nc.tensor.matmul_mx(out=y_ps[:], lhsT=hq[:].bitcast(FP8X4), lhsT_scale=hq_s[:],
+                                rhs=pw[:].bitcast(FP8X4), rhs_scale=ps[:], start=True, stop=True)
+            z_ps = psum.tile([P, U], F32, name="z_ps", bufs=3)
+            nc.tensor.matmul_mx(out=z_ps[:], lhsT=hq[:].bitcast(FP8X4), lhsT_scale=hq_s[:],
+                                rhs=nw[:].bitcast(FP8X4), rhs_scale=ns[:], start=True, stop=True)
+            y_sb = keep.tile([P, V], F32, name=f"y_sb{i}")
+            nc.scalar.activation(y_sb[:], y_ps[:], ACT.Copy)
+            diff = keep.tile([P, V, D], F32, name=f"diff{i}")
+            nc.vector.tensor_tensor(diff[:], z_ps[:].rearrange("p (v d) -> p v d", d=D),
+                                    y_sb[:].unsqueeze(2).to_broadcast([P, V, D]), ALU.subtract)
+            th = keep.tile([P, V, D], F32, name=f"th{i}")
+            nc.scalar.activation(th[:], diff[:], ACT.Tanh, scale=2.0)
+            sm = keep.tile([P, V], F32, name=f"sm{i}")
+            nc.vector.tensor_tensor(sm[:], th[:, :, 0], th[:, :, 1], ALU.add)
+            sums.append(sm)
+
+        for i in range(TILES):
+            lg = keep.tile([P, V], F32, name=f"lg{i}")
+            nc.scalar.activation(lg[:], sums[i][:], ACT.Ln, scale=0.5, bias=2.0)
+            res = keep.tile([P, V], F32, name=f"res{i}")
+            nc.vector.tensor_tensor(res[:], lg[:], gain_sb[:], ALU.mult)
+            nc.sync.dma_start(out[P * i : P * (i + 1), :], res[:])

@@ -30,7 +30,7 @@ def tile_picked_ysmap_log_p_kernel(
         neg_sb = keep.tile([P, U // 16], U16, name="neg_sb")
         pos_sb = keep.tile([P, V // 16], U16, name="pos_sb")
         xs_all = keep.tile([P, T], U8, name="xs_all", align_bytes=64)
-        es_all = keep.tile([P, W], U8, name="es_all", align_bytes=64)
+        es_all = keep.tile([P, W], U8, name="es_all", tag="es_then_hq", align_bytes=64)
         xw_all = keep.tile([P, T], I32, name="xw_all", align_bytes=64)
         ew_all = keep.tile([P, W], I32, name="ew_all", align_bytes=64)
         w_raw = [keep.tile([P, 4, H // 2], F32, name=f"w_raw{a}", align_bytes=64) for a in range(2)]
@@ -41,88 +41,100 @@ def tile_picked_ysmap_log_p_kernel(
 
         w_view = w1.rearrange("(p j) c -> p j c", j=4)
         nc.sync.dma_start(offs_sb[:], offs)
-        for q in range(4):
-            nc.scalar.dma_start(xs_all[32 * q : 32 * q + 4, :].bitcast(I32), x_scales[0, 4 * q : 4 * q + 4, :].bitcast(I32))
-        nc.sync.dma_start(neg_sb[:], neg)
-        nc.sync.dma_start(pos_sb[:], pos)
-        nc.sync.dma_start(w_raw[0][:], w_view[:, :, 0 : H // 2])
-        for q in range(4):
-            nc.scalar.dma_start(es_all[32 * q : 32 * q + 4, :].bitcast(I32), e_scales[0, 4 * q : 4 * q + 4, :].bitcast(I32))
-        nc.sync.dma_start(w_raw[1][:], w_view[:, :, H // 2 : H])
         nc.sync.dma_start(xw_all[:], x_words[0].rearrange("p n t -> p (n t)").bitcast(I32))
+        for q in range(4):
+            nc.sync.dma_start(xs_all[32 * q : 32 * q + 4, :].bitcast(I32), x_scales[0, 4 * q : 4 * q + 4, :].bitcast(I32))
+        nc.sync.dma_start(w_raw[0][:], w_view[:, :, 0 : H // 2])
+        nc.sync.dma_start(w_raw[1][:], w_view[:, :, H // 2 : H])
+        nc.sync.dma_start(pos_sb[:], pos)
+        nc.sync.dma_start(neg_sb[:], neg)
         nc.sync.dma_start(ew_all[:], e_words[0].rearrange("p n t -> p (n t)").bitcast(I32))
+        for q in range(4):
+            nc.sync.dma_start(es_all[32 * q : 32 * q + 4, :].bitcast(I32), e_scales[0, 4 * q : 4 * q + 4, :].bitcast(I32))
         nc.sync.dma_start(gain_sb[:], gain)
 
         xs = keep.tile([P, S], U8, name="xs", align_bytes=64)
         ns = keep.tile([P, U], U8, name="ns", align_bytes=64)
         ps = keep.tile([P, V], U8, name="ps", align_bytes=64)
-        xw = [keep.tile([P, P], U32, name=f"xw{i}", align_bytes=64) for i in range(TILES)]
-        nw = keep.tile([P, U], U32, name="nw", align_bytes=64)
+        xw = keep.tile([P, S], U32, name="xw", align_bytes=64)
         pw = keep.tile([P, V], U32, name="pw", align_bytes=64)
 
+        nc.vector.tensor_copy(xw[:], xw_all[:].bitcast(U32).indirect(offs_sb[:]))
         nc.vector.tensor_copy(xs[:], xs_all[:].indirect(offs_sb[:]))
-        nc.vector.tensor_copy(ns[:], es_all[:].indirect(neg_sb[:]))
-        nc.vector.tensor_copy(ps[:], es_all[:].indirect(pos_sb[:]))
 
         w_bf = keep.tile([P, 4, P, 4], BF16, name="w_bf", align_bytes=64)
-        for a in range(2):
-            nc.scalar.activation(
-                w_bf[:, :, 64 * a : 64 * a + 64, :].rearrange("p t m j -> p m t j"),
-                w_raw[a][:].rearrange("p j (m t) -> p m t j", t=4),
-                ACT.Copy,
+
+        def cast_views(m0, m1):
+            a = m0 // 64
+            return (
+                w_bf[:, :, m0:m1, :].rearrange("p t m j -> p m t j"),
+                w_raw[a][:, :, 4 * (m0 - 64 * a) : 4 * (m1 - 64 * a)].rearrange("p j (m t) -> p m t j", t=4),
             )
+
+        nc.scalar.activation(*cast_views(0, 64), ACT.Copy)
+        nc.scalar.activation(*cast_views(64, 104), ACT.Copy)
+        nc.vector.tensor_copy(*cast_views(104, P))
         wq = keep.tile([P, H], U32, name="wq", align_bytes=64)
         wq_s = keep.tile([P, H], U8, name="wq_s", align_bytes=64)
         nc.vector.quantize_mx(out=wq[:].bitcast(FP8X4), scales=wq_s[:], in_=w_bf[:].rearrange("p t m j -> p (t m j)"))
 
-        for i in range(TILES):
-            nc.vector.tensor_copy(xw[i][:], xw_all[:].bitcast(U32).indirect(offs_sb[:, 8 * i : 8 * i + 8]))
-
         h_bf = []
         for i in range(TILES):
-            h_ps = psum.tile([P, 4, P], F32, name="h_ps", bufs=3)
+            h_ps = psum.tile([P, 4, P], F32, name="h_ps", tag="wide", bufs=6)
             for t in range(4):
                 nc.tensor.matmul_mx(
                     out=h_ps[:, t, :],
                     lhsT=wq[:, P * t : P * (t + 1)].bitcast(FP8X4),
                     lhsT_scale=wq_s[:, P * t : P * (t + 1)],
-                    rhs=xw[i][:].bitcast(FP8X4),
+                    rhs=xw[:, P * i : P * (i + 1)].bitcast(FP8X4),
                     rhs_scale=xs[:, P * i : P * (i + 1)],
                     start=True,
                     stop=True,
                 )
-            hb = keep.tile([P, P, 4], BF16, name=f"h_bf{i}", align_bytes=64)
+            hb = keep.tile([P, P, 4], BF16, name=f"h_bf{i}", tag=f"h_bf{i}", align_bytes=64)
             nc.scalar.activation(hb[:], h_ps[:].rearrange("p t n -> p n t"), ACT.Copy)
             h_bf.append(hb)
 
-        nc.vector.tensor_copy(nw[:], ew_all[:].bitcast(U32).indirect(neg_sb[:]))
         nc.vector.tensor_copy(pw[:], ew_all[:].bitcast(U32).indirect(pos_sb[:]))
+        nc.vector.tensor_copy(ps[:], es_all[:].indirect(pos_sb[:]))
+        nc.vector.tensor_copy(ns[:], es_all[:].indirect(neg_sb[:]))
+
+        hq = keep.tile([P, S], U32, name="hq", tag="es_then_hq", align_bytes=64)
+        hq_s = keep.tile([P, S], U8, name="hq_s", align_bytes=64)
+        y_sb = []
+        nw = None
+        for i in range(TILES):
+            cols = slice(P * i, P * (i + 1))
+            nc.vector.quantize_mx(out=hq[:, cols].bitcast(FP8X4), scales=hq_s[:, cols], in_=h_bf[i][:].rearrange("p n t -> p (n t)"))
+            if i == 1:
+                nw = keep.tile([P, U], U32, name="nw", tag="h_bf0", align_bytes=64)
+                nc.vector.tensor_copy(nw[:], ew_all[:].bitcast(U32).indirect(neg_sb[:]))
+            y_ps = psum.tile([P, V], F32, name="y_ps", bufs=2)
+            nc.tensor.matmul_mx(out=y_ps[:], lhsT=hq[:, cols].bitcast(FP8X4), lhsT_scale=hq_s[:, cols],
+                                rhs=pw[:].bitcast(FP8X4), rhs_scale=ps[:], start=True, stop=True)
+            y_sb.append(keep.tile([P, V], F32, name=f"y_sb{i}"))
+            nc.scalar.activation(y_sb[i][:], y_ps[:], ACT.Copy)
+
+        diff, th = [], []
+        for i in range(TILES):
+            cols = slice(P * i, P * (i + 1))
+            z_ps = psum.tile([P, U], F32, name="z_ps", tag="wide", bufs=6)
+            nc.tensor.matmul_mx(out=z_ps[:], lhsT=hq[:, cols].bitcast(FP8X4), lhsT_scale=hq_s[:, cols],
+                                rhs=nw[:].bitcast(FP8X4), rhs_scale=ns[:], start=True, stop=True)
+            diff.append(keep.tile([P, V, D], F32, name=f"diff{i}", tag=f"diff{i}"))
+            nc.vector.tensor_tensor(diff[i][:], z_ps[:].rearrange("p (v d) -> p v d", d=D),
+                                    y_sb[i][:].unsqueeze(2).to_broadcast([P, V, D]), ALU.subtract)
+            th.append(keep.tile([P, V, D], F32, name=f"th{i}"))
+            nc.scalar.activation(th[i][:], diff[i][:], ACT.Tanh, scale=2.0)
 
         sums = []
         for i in range(TILES):
-            hq = keep.tile([P, P], U32, name=f"hq{i}", align_bytes=64)
-            hq_s = keep.tile([P, P], U8, name=f"hq_s{i}", align_bytes=64)
-            nc.vector.quantize_mx(out=hq[:].bitcast(FP8X4), scales=hq_s[:], in_=h_bf[i][:].rearrange("p n t -> p (n t)"))
-            y_ps = psum.tile([P, V], F32, name="y_ps", bufs=2)
-            nc.tensor.matmul_mx(out=y_ps[:], lhsT=hq[:].bitcast(FP8X4), lhsT_scale=hq_s[:],
-                                rhs=pw[:].bitcast(FP8X4), rhs_scale=ps[:], start=True, stop=True)
-            z_ps = psum.tile([P, U], F32, name="z_ps", bufs=3)
-            nc.tensor.matmul_mx(out=z_ps[:], lhsT=hq[:].bitcast(FP8X4), lhsT_scale=hq_s[:],
-                                rhs=nw[:].bitcast(FP8X4), rhs_scale=ns[:], start=True, stop=True)
-            y_sb = keep.tile([P, V], F32, name=f"y_sb{i}")
-            nc.scalar.activation(y_sb[:], y_ps[:], ACT.Copy)
-            diff = keep.tile([P, V, D], F32, name=f"diff{i}")
-            nc.vector.tensor_tensor(diff[:], z_ps[:].rearrange("p (v d) -> p v d", d=D),
-                                    y_sb[:].unsqueeze(2).to_broadcast([P, V, D]), ALU.subtract)
-            th = keep.tile([P, V, D], F32, name=f"th{i}")
-            nc.scalar.activation(th[:], diff[:], ACT.Tanh, scale=2.0)
-            sm = keep.tile([P, V], F32, name=f"sm{i}")
-            nc.vector.tensor_tensor(sm[:], th[:, :, 0], th[:, :, 1], ALU.add)
-            sums.append(sm)
+            sums.append(keep.tile([P, V], F32, name=f"sm{i}"))
+            nc.vector.tensor_tensor(sums[i][:], th[i][:, :, 0], th[i][:, :, 1], ALU.add)
 
+        lg = keep.tile([P, TILES * V], F32, name="lg", tag=f"diff{TILES - 1}")
         for i in range(TILES):
-            lg = keep.tile([P, V], F32, name=f"lg{i}")
-            nc.scalar.activation(lg[:], sums[i][:], ACT.Ln, scale=0.5, bias=2.0)
+            nc.scalar.activation(lg[:, V * i : V * (i + 1)], sums[i][:], ACT.Ln, scale=0.5, bias=2.0)
             res = keep.tile([P, V], F32, name=f"res{i}")
-            nc.vector.tensor_tensor(res[:], lg[:], gain_sb[:], ALU.mult)
+            nc.vector.tensor_tensor(res[:], lg[:, V * i : V * (i + 1)], gain_sb[:], ALU.mult)
             nc.sync.dma_start(out[P * i : P * (i + 1), :], res[:])

@@ -40,17 +40,18 @@ def tile_picked_ysmap_log_p_kernel(
         nc.vector.memset(es_all[:].bitcast(I32), 0)
 
         w_view = w1.rearrange("(p j) c -> p j c", j=4)
-        nc.sync.dma_start(offs_sb[:], offs)
         nc.sync.dma_start(xw_all[:], x_words[0].rearrange("p n t -> p (n t)").bitcast(I32))
+        nc.sync.dma_start(offs_sb[:], offs)
         for q in range(4):
-            nc.sync.dma_start(xs_all[32 * q : 32 * q + 4, :].bitcast(I32), x_scales[0, 4 * q : 4 * q + 4, :].bitcast(I32))
+            nc.sync.dma_start(xs_all[q:P:32, :].bitcast(I32), x_scales[0, q:16:4, :].bitcast(I32))
         nc.sync.dma_start(w_raw[0][:], w_view[:, :, 0 : H // 2])
         nc.sync.dma_start(w_raw[1][:], w_view[:, :, H // 2 : H])
         nc.sync.dma_start(pos_sb[:], pos)
-        nc.sync.dma_start(neg_sb[:], neg)
-        nc.sync.dma_start(ew_all[:], e_words[0].rearrange("p n t -> p (n t)").bitcast(I32))
         for q in range(4):
-            nc.sync.dma_start(es_all[32 * q : 32 * q + 4, :].bitcast(I32), e_scales[0, 4 * q : 4 * q + 4, :].bitcast(I32))
+            if q == 1:
+                nc.sync.dma_start(ew_all[:], e_words[0].rearrange("p n t -> p (n t)").bitcast(I32))
+            nc.sync.dma_start(es_all[q:P:32, :].bitcast(I32), e_scales[0, q:16:4, :].bitcast(I32))
+        nc.sync.dma_start(neg_sb[:], neg)
         nc.sync.dma_start(gain_sb[:], gain)
 
         xs = keep.tile([P, S], U8, name="xs", align_bytes=64)
@@ -72,8 +73,8 @@ def tile_picked_ysmap_log_p_kernel(
             )
 
         nc.scalar.activation(*cast_views(0, 64), ACT.Copy)
-        nc.scalar.activation(*cast_views(64, 104), ACT.Copy)
-        nc.vector.tensor_copy(*cast_views(104, P))
+        nc.scalar.activation(*cast_views(64, 88), ACT.Copy)
+        nc.vector.tensor_copy(*cast_views(88, P))
         wq = keep.tile([P, H], U32, name="wq", align_bytes=64)
         wq_s = keep.tile([P, H], U8, name="wq_s", align_bytes=64)
         nc.vector.quantize_mx(out=wq[:].bitcast(FP8X4), scales=wq_s[:], in_=w_bf[:].rearrange("p t m j -> p (t m j)"))
@@ -99,42 +100,55 @@ def tile_picked_ysmap_log_p_kernel(
         nc.vector.tensor_copy(ps[:], es_all[:].indirect(pos_sb[:]))
         nc.vector.tensor_copy(ns[:], es_all[:].indirect(neg_sb[:]))
 
+        nw = [keep.tile([P, V], U32, name="nw0", align_bytes=64)]
+        nc.vector.tensor_copy(nw[0][:], ew_all[:].bitcast(U32).indirect(neg_sb[:, 0:16]))
+
         hq = keep.tile([P, S], U32, name="hq", tag="es_then_hq", align_bytes=64)
         hq_s = keep.tile([P, S], U8, name="hq_s", align_bytes=64)
+        HALF = V // 2
+
+        def second_product(dst, i, words, scales):
+            cols = slice(P * i, P * (i + 1))
+            nc.tensor.matmul_mx(out=dst, lhsT=hq[:, cols].bitcast(FP8X4), lhsT_scale=hq_s[:, cols],
+                                rhs=words.bitcast(FP8X4), rhs_scale=scales, start=True, stop=True)
+
         y_sb = []
-        nw = None
         for i in range(TILES):
             cols = slice(P * i, P * (i + 1))
             nc.vector.quantize_mx(out=hq[:, cols].bitcast(FP8X4), scales=hq_s[:, cols], in_=h_bf[i][:].rearrange("p n t -> p (n t)"))
-            if i == 1:
-                nw = keep.tile([P, U], U32, name="nw", tag="h_bf0", align_bytes=64)
-                nc.vector.tensor_copy(nw[:], ew_all[:].bitcast(U32).indirect(neg_sb[:]))
             y_ps = psum.tile([P, V], F32, name="y_ps", bufs=2)
-            nc.tensor.matmul_mx(out=y_ps[:], lhsT=hq[:, cols].bitcast(FP8X4), lhsT_scale=hq_s[:, cols],
-                                rhs=pw[:].bitcast(FP8X4), rhs_scale=ps[:], start=True, stop=True)
+            second_product(y_ps[:], i, pw[:], ps[:])
             y_sb.append(keep.tile([P, V], F32, name=f"y_sb{i}"))
             nc.scalar.activation(y_sb[i][:], y_ps[:], ACT.Copy)
 
-        diff, th = [], []
-        for i in range(TILES):
-            cols = slice(P * i, P * (i + 1))
-            z_ps = psum.tile([P, U], F32, name="z_ps", tag="wide", bufs=6)
-            nc.tensor.matmul_mx(out=z_ps[:], lhsT=hq[:, cols].bitcast(FP8X4), lhsT_scale=hq_s[:, cols],
-                                rhs=nw[:].bitcast(FP8X4), rhs_scale=ns[:], start=True, stop=True)
-            diff.append(keep.tile([P, V, D], F32, name=f"diff{i}", tag=f"diff{i}"))
-            nc.vector.tensor_tensor(diff[i][:], z_ps[:].rearrange("p (v d) -> p v d", d=D),
-                                    y_sb[i][:].unsqueeze(2).to_broadcast([P, V, D]), ALU.subtract)
-            th.append(keep.tile([P, V, D], F32, name=f"th{i}"))
-            nc.scalar.activation(th[i][:], diff[i][:], ACT.Tanh, scale=2.0)
+        nw.append(keep.tile([P, V], U32, name="nw1", tag="h_bf2", align_bytes=64))
+        nc.vector.tensor_copy(nw[1][:], ew_all[:].bitcast(U32).indirect(neg_sb[:, 16:32]))
 
-        sums = []
-        for i in range(TILES):
-            sums.append(keep.tile([P, V], F32, name=f"sm{i}"))
-            nc.vector.tensor_tensor(sums[i][:], th[i][:, :, 0], th[i][:, :, 1], ALU.add)
+        pieces = []
+        for half in range(2):
+            for g in range(2):
+                z_ps = psum.tile([P, 2, V], F32, name="z_ps", tag="wide", bufs=6)
+                for r in range(2):
+                    second_product(z_ps[:, r, :], 2 * g + r, nw[half][:], ns[:, V * half : V * (half + 1)])
+                for r in range(2):
+                    i = 2 * g + r
+                    diff = keep.tile([P, HALF, D], F32, name=f"diff{len(pieces)}", tag=f"diff{len(pieces)}")
+                    nc.vector.tensor_tensor(diff[:], z_ps[:, r, :].rearrange("p (v d) -> p v d", d=D),
+                                            y_sb[i][:, HALF * half : HALF * (half + 1)].unsqueeze(2).to_broadcast([P, HALF, D]), ALU.subtract)
+                    if half == 0:
+                        pieces.append(keep.tile([P, V, D], F32, name=f"th{i}"))
+                    else:
+                        pieces.append(None)
+                    nc.scalar.activation(pieces[i][:, HALF * half : HALF * (half + 1), :], diff[:], ACT.Tanh, scale=2.0)
 
-        lg = keep.tile([P, TILES * V], F32, name="lg", tag=f"diff{TILES - 1}")
+        sums = [keep.tile([P, V], F32, name=f"sums{i}") for i in range(TILES)]
         for i in range(TILES):
-            nc.scalar.activation(lg[:, V * i : V * (i + 1)], sums[i][:], ACT.Ln, scale=0.5, bias=2.0)
-            res = keep.tile([P, V], F32, name=f"res{i}")
-            nc.vector.tensor_tensor(res[:], lg[:, V * i : V * (i + 1)], gain_sb[:], ALU.mult)
-            nc.sync.dma_start(out[P * i : P * (i + 1), :], res[:])
+            nc.vector.tensor_tensor(sums[i][:], pieces[i][:, :, 0], pieces[i][:, :, 1], ALU.add)
+
+        lg = keep.tile([P, TILES * V], F32, name="lg", tag=f"diff{len(pieces) - 1}")
+        for i in range(TILES):
+            for c0, c1 in ([(0, HALF), (HALF, V)] if i == TILES - 1 else [(0, V)]):
+                nc.scalar.activation(lg[:, V * i + c0 : V * i + c1], sums[i][:, c0:c1], ACT.Ln, scale=0.5, bias=2.0)
+                res = keep.tile([P, c1 - c0], F32, name=f"res{i}_{c0}")
+                nc.vector.tensor_tensor(res[:], lg[:, V * i + c0 : V * i + c1], gain_sb[:, c0:c1], ALU.mult)
+                nc.sync.dma_start(out[P * i : P * (i + 1), c0:c1], res[:])

@@ -29,41 +29,45 @@ def tile_picked_ysmap_log_p_kernel(
         offs_sb = keep.tile([P, S // 16], U16, name="offs_sb")
         neg_sb = keep.tile([P, U // 16], U16, name="neg_sb")
         pos_sb = keep.tile([P, V // 16], U16, name="pos_sb")
-        xs_all = keep.tile([P, T], U8, name="xs_all", align_bytes=64)
-        es_all = keep.tile([P, W], U8, name="es_all", tag="es_then_hq", align_bytes=64)
+        xs_all = keep.tile([P, T], U8, name="xs_all", tag="xs_then_wq", align_bytes=64)
+        es_all = keep.tile([P, W], U8, name="es_all", align_bytes=64)
         xw_all = keep.tile([P, T], I32, name="xw_all", align_bytes=64)
         ew_all = keep.tile([P, W], I32, name="ew_all", align_bytes=64)
-        w_raw = [keep.tile([P, 4, H // 2], F32, name=f"w_raw{a}", align_bytes=64) for a in range(2)]
+        w_raw = [keep.tile([P, 4, H // 2], F32, name=f"w_raw{a}", tag=f"w_raw{a}", align_bytes=64) for a in range(2)]
         gain_sb = keep.tile([P, V], F32, name="gain_sb")
 
-        nc.vector.memset(xs_all[:].bitcast(I32), 0)
         nc.vector.memset(es_all[:].bitcast(I32), 0)
+        nc.gpsimd.memset(xs_all[:].bitcast(I32), 0)
+
+        def load_scale_rows(plane, rows, q):
+            nc.sync.dma_start(plane[q:P:32, :].bitcast(I32), rows[0, q:16:4, :].bitcast(I32))
 
         w_view = w1.rearrange("(p j) c -> p j c", j=4)
-        nc.sync.dma_start(xw_all[:], x_words[0].rearrange("p n t -> p (n t)").bitcast(I32))
-        nc.sync.dma_start(offs_sb[:], offs)
-        for q in range(4):
-            nc.sync.dma_start(xs_all[q:P:32, :].bitcast(I32), x_scales[0, q:16:4, :].bitcast(I32))
-        nc.sync.dma_start(w_raw[0][:], w_view[:, :, 0 : H // 2])
-        nc.sync.dma_start(w_raw[1][:], w_view[:, :, H // 2 : H])
-        nc.sync.dma_start(pos_sb[:], pos)
-        for q in range(4):
-            if q == 1:
-                nc.sync.dma_start(ew_all[:], e_words[0].rearrange("p n t -> p (n t)").bitcast(I32))
-            nc.sync.dma_start(es_all[q:P:32, :].bitcast(I32), e_scales[0, q:16:4, :].bitcast(I32))
         nc.sync.dma_start(neg_sb[:], neg)
+        nc.sync.dma_start(w_raw[0][:], w_view[:, :, 0 : H // 2])
+        for q in range(4):
+            load_scale_rows(es_all, e_scales, q)
+        nc.sync.dma_start(offs_sb[:], offs)
+        nc.sync.dma_start(xw_all[:], x_words[0].rearrange("p n t -> p (n t)").bitcast(I32))
+        nc.sync.dma_start(w_raw[1][:], w_view[:, :, H // 2 : H])
+        for q in range(4):
+            load_scale_rows(xs_all, x_scales, q)
+        nc.sync.dma_start(pos_sb[:], pos)
+        nc.sync.dma_start(ew_all[:], e_words[0].rearrange("p n t -> p (n t)").bitcast(I32))
         nc.sync.dma_start(gain_sb[:], gain)
 
         xs = keep.tile([P, S], U8, name="xs", align_bytes=64)
-        ns = keep.tile([P, U], U8, name="ns", align_bytes=64)
+        ns_listed = keep.tile([P, U], U8, name="ns_listed", align_bytes=64)
         ps = keep.tile([P, V], U8, name="ps", align_bytes=64)
         xw = keep.tile([P, S], U32, name="xw", align_bytes=64)
         pw = keep.tile([P, V], U32, name="pw", align_bytes=64)
+        nw = keep.tile([P, D, V], U32, name="nw", align_bytes=64)
 
+        nc.vector.tensor_copy(ns_listed[:], es_all[:].indirect(neg_sb[:]))
         nc.vector.tensor_copy(xw[:], xw_all[:].bitcast(U32).indirect(offs_sb[:]))
         nc.vector.tensor_copy(xs[:], xs_all[:].indirect(offs_sb[:]))
 
-        w_bf = keep.tile([P, 4, P, 4], BF16, name="w_bf", align_bytes=64)
+        w_bf = keep.tile([P, 4, P, 4], BF16, name="w_bf", tag="w_then_ns", align_bytes=64)
 
         def cast_views(m0, m1):
             a = m0 // 64
@@ -73,15 +77,17 @@ def tile_picked_ysmap_log_p_kernel(
             )
 
         nc.scalar.activation(*cast_views(0, 64), ACT.Copy)
-        nc.scalar.activation(*cast_views(64, 88), ACT.Copy)
-        nc.vector.tensor_copy(*cast_views(88, P))
-        wq = keep.tile([P, H], U32, name="wq", align_bytes=64)
+        nc.scalar.activation(*cast_views(64, P), ACT.Copy)
+        wq = keep.tile([P, H], U32, name="wq", tag="xs_then_wq", align_bytes=64)
         wq_s = keep.tile([P, H], U8, name="wq_s", align_bytes=64)
         nc.vector.quantize_mx(out=wq[:].bitcast(FP8X4), scales=wq_s[:], in_=w_bf[:].rearrange("p t m j -> p (t m j)"))
+        nc.vector.tensor_copy(ps[:], es_all[:].indirect(pos_sb[:]))
+        ns = keep.tile([P, D, V], U8, name="ns", tag="w_then_ns", align_bytes=64)
+        nc.vector.tensor_copy(ns[:], ns_listed[:].rearrange("p (v d) -> p d v", d=D))
 
         h_bf = []
         for i in range(TILES):
-            h_ps = psum.tile([P, 4, P], F32, name="h_ps", tag="wide", bufs=6)
+            h_ps = psum.tile([P, 4, P], F32, name="h_ps", tag="bank", bufs=8)
             for t in range(4):
                 nc.tensor.matmul_mx(
                     out=h_ps[:, t, :],
@@ -92,63 +98,44 @@ def tile_picked_ysmap_log_p_kernel(
                     start=True,
                     stop=True,
                 )
-            hb = keep.tile([P, P, 4], BF16, name=f"h_bf{i}", tag=f"h_bf{i}", align_bytes=64)
+            hb = keep.tile([P, P, 4], BF16, name=f"h_bf{i}", align_bytes=64)
             nc.scalar.activation(hb[:], h_ps[:].rearrange("p t n -> p n t"), ACT.Copy)
             h_bf.append(hb)
 
         nc.vector.tensor_copy(pw[:], ew_all[:].bitcast(U32).indirect(pos_sb[:]))
-        nc.vector.tensor_copy(ps[:], es_all[:].indirect(pos_sb[:]))
-        nc.vector.tensor_copy(ns[:], es_all[:].indirect(neg_sb[:]))
+        nc.vector.tensor_copy(nw[:].rearrange("p d v -> p v d"), ew_all[:].bitcast(U32).indirect(neg_sb[:]))
 
-        nw = [keep.tile([P, V], U32, name="nw0", align_bytes=64)]
-        nc.vector.tensor_copy(nw[0][:], ew_all[:].bitcast(U32).indirect(neg_sb[:, 0:16]))
+        def quantize(name, codes, values):
+            scales = keep.tile([P, P], U8, name=name + "_s", align_bytes=64)
+            nc.vector.quantize_mx(out=codes[:].bitcast(FP8X4), scales=scales[:], in_=values[:].rearrange("p n t -> p (n t)"))
+            return scales
 
-        hq = keep.tile([P, S], U32, name="hq", tag="es_then_hq", align_bytes=64)
-        hq_s = keep.tile([P, S], U8, name="hq_s", align_bytes=64)
+        th = keep.tile([P, TILES, D, V], F32, name="th")
+        for i in range(TILES):
+            minus_h = keep.tile([P, P, 4], BF16, name=f"minus_h{i}", align_bytes=64)
+            mq = keep.tile([P, P], U32, name=f"mq{i}", align_bytes=64)
+            nc.vector.tensor_scalar(minus_h[:], h_bf[i][:], -1.0, None, ALU.mult)
+            hq = keep.tile([P, P], U32, name=f"hq{i}", align_bytes=64)
+            hq_s = quantize(f"hq{i}", hq, h_bf[i])
+            mq_s = quantize(f"mq{i}", mq, minus_h)
+            for members in ([(0,), (1,)] if i in (0, TILES - 1) else [(0, 1)]):
+              z_ps = psum.tile([P, D, V], F32, name="z_ps", tag="bank", bufs=8)
+              for d in members:
+                nc.tensor.matmul_mx(out=z_ps[:, d, :], lhsT=hq[:].bitcast(FP8X4), lhsT_scale=hq_s[:],
+                                    rhs=nw[:, d, :].bitcast(FP8X4), rhs_scale=ns[:, d, :], start=True, stop=False)
+                nc.tensor.matmul_mx(out=z_ps[:, d, :], lhsT=mq[:].bitcast(FP8X4), lhsT_scale=mq_s[:],
+                                    rhs=pw[:].bitcast(FP8X4), rhs_scale=ps[:], start=False, stop=True)
+              ds = slice(members[0], members[-1] + 1)
+              nc.scalar.activation(th[:, i, ds, :], z_ps[:, ds, :], ACT.Tanh, scale=2.0)
+
+        sums = keep.tile([P, TILES, V], F32, name="sums")
+        nc.vector.tensor_tensor(sums[:], th[:, :, 0, :], th[:, :, 1, :], ALU.add)
+
         HALF = V // 2
-
-        def second_product(dst, i, words, scales):
-            cols = slice(P * i, P * (i + 1))
-            nc.tensor.matmul_mx(out=dst, lhsT=hq[:, cols].bitcast(FP8X4), lhsT_scale=hq_s[:, cols],
-                                rhs=words.bitcast(FP8X4), rhs_scale=scales, start=True, stop=True)
-
-        y_sb = []
-        for i in range(TILES):
-            cols = slice(P * i, P * (i + 1))
-            nc.vector.quantize_mx(out=hq[:, cols].bitcast(FP8X4), scales=hq_s[:, cols], in_=h_bf[i][:].rearrange("p n t -> p (n t)"))
-            y_ps = psum.tile([P, V], F32, name="y_ps", bufs=2)
-            second_product(y_ps[:], i, pw[:], ps[:])
-            y_sb.append(keep.tile([P, V], F32, name=f"y_sb{i}"))
-            nc.scalar.activation(y_sb[i][:], y_ps[:], ACT.Copy)
-
-        nw.append(keep.tile([P, V], U32, name="nw1", tag="h_bf2", align_bytes=64))
-        nc.vector.tensor_copy(nw[1][:], ew_all[:].bitcast(U32).indirect(neg_sb[:, 16:32]))
-
-        pieces = []
-        for half in range(2):
-            for g in range(2):
-                z_ps = psum.tile([P, 2, V], F32, name="z_ps", tag="wide", bufs=6)
-                for r in range(2):
-                    second_product(z_ps[:, r, :], 2 * g + r, nw[half][:], ns[:, V * half : V * (half + 1)])
-                for r in range(2):
-                    i = 2 * g + r
-                    diff = keep.tile([P, HALF, D], F32, name=f"diff{len(pieces)}", tag=f"diff{len(pieces)}")
-                    nc.vector.tensor_tensor(diff[:], z_ps[:, r, :].rearrange("p (v d) -> p v d", d=D),
-                                            y_sb[i][:, HALF * half : HALF * (half + 1)].unsqueeze(2).to_broadcast([P, HALF, D]), ALU.subtract)
-                    if half == 0:
-                        pieces.append(keep.tile([P, V, D], F32, name=f"th{i}"))
-                    else:
-                        pieces.append(None)
-                    nc.scalar.activation(pieces[i][:, HALF * half : HALF * (half + 1), :], diff[:], ACT.Tanh, scale=2.0)
-
-        sums = [keep.tile([P, V], F32, name=f"sums{i}") for i in range(TILES)]
-        for i in range(TILES):
-            nc.vector.tensor_tensor(sums[i][:], pieces[i][:, :, 0], pieces[i][:, :, 1], ALU.add)
-
-        lg = keep.tile([P, TILES * V], F32, name="lg", tag=f"diff{len(pieces) - 1}")
         for i in range(TILES):
             for c0, c1 in ([(0, HALF), (HALF, V)] if i == TILES - 1 else [(0, V)]):
-                nc.scalar.activation(lg[:, V * i + c0 : V * i + c1], sums[i][:, c0:c1], ACT.Ln, scale=0.5, bias=2.0)
+                lg = keep.tile([P, c1 - c0], F32, name=f"lg{i}_{c0}")
+                nc.scalar.activation(lg[:], sums[:, i, c0:c1], ACT.Ln, scale=0.5, bias=2.0)
                 res = keep.tile([P, c1 - c0], F32, name=f"res{i}_{c0}")
-                nc.vector.tensor_tensor(res[:], lg[:, V * i + c0 : V * i + c1], gain_sb[:, c0:c1], ALU.mult)
+                nc.vector.tensor_tensor(res[:], lg[:], gain_sb[:, c0:c1], ALU.mult)
                 nc.sync.dma_start(out[P * i : P * (i + 1), c0:c1], res[:])

@@ -15,6 +15,7 @@ ALU = mybir.AluOpType
 P = 128
 K, T, S, H, D, V, W, U = 512, 1024, 512, 512, 2, 256, 1024, 512
 TILES = S // P
+SCALAR_NEGATES = 1
 FLOPS = 2 * K * H * S + 2 * H * S * U + 2 * H * S * V
 
 
@@ -29,7 +30,7 @@ def tile_picked_ysmap_log_p_kernel(
         offs_sb = keep.tile([P, S // 16], U16, name="offs_sb")
         neg_sb = keep.tile([P, U // 16], U16, name="neg_sb")
         pos_sb = keep.tile([P, V // 16], U16, name="pos_sb")
-        xs_all = keep.tile([P, T], U8, name="xs_all", tag="xs_then_wq", align_bytes=64)
+        xs_all = keep.tile([P, T], U8, name="xs_all", align_bytes=64)
         es_all = keep.tile([P, W], U8, name="es_all", align_bytes=64)
         xw_all = keep.tile([P, T], I32, name="xw_all", align_bytes=64)
         ew_all = keep.tile([P, W], I32, name="ew_all", align_bytes=64)
@@ -45,14 +46,14 @@ def tile_picked_ysmap_log_p_kernel(
         w_view = w1.rearrange("(p j) c -> p j c", j=4)
         nc.sync.dma_start(neg_sb[:], neg)
         nc.sync.dma_start(w_raw[0][:], w_view[:, :, 0 : H // 2])
+        nc.sync.dma_start(pos_sb[:], pos)
         for q in range(4):
             load_scale_rows(es_all, e_scales, q)
-        nc.sync.dma_start(offs_sb[:], offs)
-        nc.sync.dma_start(xw_all[:], x_words[0].rearrange("p n t -> p (n t)").bitcast(I32))
         nc.sync.dma_start(w_raw[1][:], w_view[:, :, H // 2 : H])
+        nc.sync.dma_start(xw_all[:], x_words[0].rearrange("p n t -> p (n t)").bitcast(I32))
         for q in range(4):
             load_scale_rows(xs_all, x_scales, q)
-        nc.sync.dma_start(pos_sb[:], pos)
+        nc.sync.dma_start(offs_sb[:], offs)
         nc.sync.dma_start(ew_all[:], e_words[0].rearrange("p n t -> p (n t)").bitcast(I32))
         nc.sync.dma_start(gain_sb[:], gain)
 
@@ -63,29 +64,32 @@ def tile_picked_ysmap_log_p_kernel(
         pw = keep.tile([P, V], U32, name="pw", align_bytes=64)
         nw = keep.tile([P, D, V], U32, name="nw", align_bytes=64)
 
+        ns = keep.tile([P, D, V], U8, name="ns", align_bytes=64)
         nc.vector.tensor_copy(ns_listed[:], es_all[:].indirect(neg_sb[:]))
-        nc.vector.tensor_copy(xw[:], xw_all[:].bitcast(U32).indirect(offs_sb[:]))
-        nc.vector.tensor_copy(xs[:], xs_all[:].indirect(offs_sb[:]))
+        nc.vector.tensor_copy(ps[:], es_all[:].indirect(pos_sb[:]))
+        nc.vector.tensor_copy(ns[:], ns_listed[:].rearrange("p (v d) -> p d v", d=D))
 
-        w_bf = keep.tile([P, 4, P, 4], BF16, name="w_bf", tag="w_then_ns", align_bytes=64)
+        w_bf = keep.tile([P, 4, P, 4], BF16, name="w_bf", align_bytes=64)
 
         def cast_views(m0, m1):
             a = m0 // 64
             return (
-                w_bf[:, :, m0:m1, :].rearrange("p t m j -> p m t j"),
-                w_raw[a][:, :, 4 * (m0 - 64 * a) : 4 * (m1 - 64 * a)].rearrange("p j (m t) -> p m t j", t=4),
+                w_bf[:, :, m0:m1, :].rearrange("p t m j -> p m j t"),
+                w_raw[a][:, :, 4 * (m0 - 64 * a) : 4 * (m1 - 64 * a)].rearrange("p j (m t) -> p m j t", t=4),
             )
 
-        nc.scalar.activation(*cast_views(0, 64), ACT.Copy)
+        nc.vector.tensor_copy(*cast_views(48, 64))
+        nc.scalar.activation(*cast_views(0, 48), ACT.Copy)
         nc.scalar.activation(*cast_views(64, P), ACT.Copy)
-        wq = keep.tile([P, H], U32, name="wq", tag="xs_then_wq", align_bytes=64)
+        wq = keep.tile([P, H], U32, name="wq", align_bytes=64)
         wq_s = keep.tile([P, H], U8, name="wq_s", align_bytes=64)
         nc.vector.quantize_mx(out=wq[:].bitcast(FP8X4), scales=wq_s[:], in_=w_bf[:].rearrange("p t m j -> p (t m j)"))
-        nc.vector.tensor_copy(ps[:], es_all[:].indirect(pos_sb[:]))
-        ns = keep.tile([P, D, V], U8, name="ns", tag="w_then_ns", align_bytes=64)
-        nc.vector.tensor_copy(ns[:], ns_listed[:].rearrange("p (v d) -> p d v", d=D))
+        for c0, c1 in [(0, S // 2), (S // 2, S)]:
+            nc.vector.tensor_copy(xw[:, c0:c1], xw_all[:].bitcast(U32).indirect(offs_sb[:, c0 // 16 : c1 // 16]))
+            nc.vector.tensor_copy(xs[:, c0:c1], xs_all[:].indirect(offs_sb[:, c0 // 16 : c1 // 16]))
 
         h_bf = []
+        minus = []
         for i in range(TILES):
             h_ps = psum.tile([P, 4, P], F32, name="h_ps", tag="bank", bufs=8)
             for t in range(4):
@@ -101,6 +105,9 @@ def tile_picked_ysmap_log_p_kernel(
             hb = keep.tile([P, P, 4], BF16, name=f"h_bf{i}", align_bytes=64)
             nc.scalar.activation(hb[:], h_ps[:].rearrange("p t n -> p n t"), ACT.Copy)
             h_bf.append(hb)
+            minus.append(keep.tile([P, P, 4], BF16, name=f"minus_h{i}", align_bytes=64))
+            if i < SCALAR_NEGATES:
+                nc.scalar.activation(minus[i][:], h_ps[:].rearrange("p t n -> p n t"), ACT.Copy, scale=-1.0)
 
         nc.vector.tensor_copy(pw[:], ew_all[:].bitcast(U32).indirect(pos_sb[:]))
         nc.vector.tensor_copy(nw[:].rearrange("p d v -> p v d"), ew_all[:].bitcast(U32).indirect(neg_sb[:]))
@@ -112,9 +119,10 @@ def tile_picked_ysmap_log_p_kernel(
 
         th = keep.tile([P, TILES, D, V], F32, name="th")
         for i in range(TILES):
-            minus_h = keep.tile([P, P, 4], BF16, name=f"minus_h{i}", align_bytes=64)
+            minus_h = minus[i]
             mq = keep.tile([P, P], U32, name=f"mq{i}", align_bytes=64)
-            nc.vector.tensor_scalar(minus_h[:], h_bf[i][:], -1.0, None, ALU.mult)
+            if i >= SCALAR_NEGATES:
+                nc.vector.tensor_scalar(minus_h[:], h_bf[i][:], -1.0, None, ALU.mult)
             hq = keep.tile([P, P], U32, name=f"hq{i}", align_bytes=64)
             hq_s = quantize(f"hq{i}", hq, h_bf[i])
             mq_s = quantize(f"mq{i}", mq, minus_h)
@@ -133,7 +141,7 @@ def tile_picked_ysmap_log_p_kernel(
 
         HALF = V // 2
         for i in range(TILES):
-            for c0, c1 in ([(0, HALF), (HALF, V)] if i == TILES - 1 else [(0, V)]):
+            for c0, c1 in ([(0, HALF), (HALF, V)] if i in (0, TILES - 1) else [(0, V)]):
                 lg = keep.tile([P, c1 - c0], F32, name=f"lg{i}_{c0}")
                 nc.scalar.activation(lg[:], sums[:, i, c0:c1], ACT.Ln, scale=0.5, bias=2.0)
                 res = keep.tile([P, c1 - c0], F32, name=f"res{i}_{c0}")

@@ -31,14 +31,14 @@ def tile_picked_ysmap_log_p_kernel(
         neg_sb = keep.tile([P, U // 16], U16, name="neg_sb")
         pos_sb = keep.tile([P, V // 16], U16, name="pos_sb")
         xs_all = keep.tile([P, T], U8, name="xs_all", align_bytes=64)
-        es_all = keep.tile([P, W], U8, name="es_all", align_bytes=64)
+        es_all = keep.tile([P, W], U8, name="es_all", tag="es_then_wq", align_bytes=64)
         xw_all = keep.tile([P, T], I32, name="xw_all", align_bytes=64)
         ew_all = keep.tile([P, W], I32, name="ew_all", align_bytes=64)
         w_raw = [keep.tile([P, 4, H // 2], F32, name=f"w_raw{a}", tag=f"w_raw{a}", align_bytes=64) for a in range(2)]
         gain_sb = keep.tile([P, V], F32, name="gain_sb")
 
         nc.vector.memset(es_all[:].bitcast(I32), 0)
-        nc.gpsimd.memset(xs_all[:].bitcast(I32), 0)
+        nc.vector.memset(xs_all[:].bitcast(I32), 0)
 
         def load_scale_rows(plane, rows, q):
             nc.sync.dma_start(plane[q:P:32, :].bitcast(I32), rows[0, q:16:4, :].bitcast(I32))
@@ -69,21 +69,24 @@ def tile_picked_ysmap_log_p_kernel(
         nc.vector.tensor_copy(ps[:], es_all[:].indirect(pos_sb[:]))
         nc.vector.tensor_copy(ns[:], ns_listed[:].rearrange("p (v d) -> p d v", d=D))
 
-        w_bf = keep.tile([P, 4, P, 4], BF16, name="w_bf", align_bytes=64)
+        w_bf = [keep.tile([P, 4, 64, 4], BF16, name=f"w_bf{a}", align_bytes=64) for a in range(2)]
 
         def cast_views(m0, m1):
             a = m0 // 64
             return (
-                w_bf[:, :, m0:m1, :].rearrange("p t m j -> p m j t"),
+                w_bf[a][:, :, m0 - 64 * a : m1 - 64 * a, :].rearrange("p t m j -> p m j t"),
                 w_raw[a][:, :, 4 * (m0 - 64 * a) : 4 * (m1 - 64 * a)].rearrange("p j (m t) -> p m j t", t=4),
             )
 
         nc.vector.tensor_copy(*cast_views(48, 64))
         nc.scalar.activation(*cast_views(0, 48), ACT.Copy)
         nc.scalar.activation(*cast_views(64, P), ACT.Copy)
-        wq = keep.tile([P, H], U32, name="wq", align_bytes=64)
+        wq = keep.tile([P, H], U32, name="wq", tag="es_then_wq", align_bytes=64)
         wq_s = keep.tile([P, H], U8, name="wq_s", align_bytes=64)
-        nc.vector.quantize_mx(out=wq[:].bitcast(FP8X4), scales=wq_s[:], in_=w_bf[:].rearrange("p t m j -> p (t m j)"))
+        for a in range(2):
+            for t in range(4):
+                cols = slice(P * t + 64 * a, P * t + 64 * (a + 1))
+                nc.vector.quantize_mx(out=wq[:, cols].bitcast(FP8X4), scales=wq_s[:, cols], in_=w_bf[a][:, t, :, :].rearrange("p m j -> p (m j)"))
         for c0, c1 in [(0, S // 2), (S // 2, S)]:
             nc.vector.tensor_copy(xw[:, c0:c1], xw_all[:].bitcast(U32).indirect(offs_sb[:, c0 // 16 : c1 // 16]))
             nc.vector.tensor_copy(xs[:, c0:c1], xs_all[:].indirect(offs_sb[:, c0 // 16 : c1 // 16]))

@@ -38,7 +38,7 @@ def tile_picked_ysmap_log_p_kernel(
         gain_sb = keep.tile([P, V], F32, name="gain_sb")
 
         nc.vector.memset(es_all[:].bitcast(I32), 0)
-        nc.vector.memset(xs_all[:].bitcast(I32), 0)
+        nc.gpsimd.memset(xs_all[:].bitcast(I32), 0)
 
         def load_scale_rows(plane, rows, q):
             nc.sync.dma_start(plane[q:P:32, :].bitcast(I32), rows[0, q:16:4, :].bitcast(I32))

@@ -15,6 +15,9 @@ ALU = mybir.AluOpType
 P = 128
 K, T, S, H, D, V, W, U = 512, 1024, 512, 512, 2, 256, 1024, 512
 TILES = S // P
+ROWS = 16
+ROW0 = P - ROWS
+W_SPLIT = 48
 SCALAR_NEGATES = 1
 FLOPS = 2 * K * H * S + 2 * H * S * U + 2 * H * S * V
 
@@ -31,68 +34,80 @@ def tile_picked_ysmap_log_p_kernel(
         neg_sb = keep.tile([P, U // 16], U16, name="neg_sb")
         pos_sb = keep.tile([P, V // 16], U16, name="pos_sb")
         xs_all = keep.tile([P, T], U8, name="xs_all", align_bytes=64)
-        es_all = keep.tile([P, W], U8, name="es_all", tag="es_then_wq", align_bytes=64)
+        es_all = keep.tile([P, W], U8, name="es_all", align_bytes=64)
         xw_all = keep.tile([P, T], I32, name="xw_all", align_bytes=64)
         ew_all = keep.tile([P, W], I32, name="ew_all", align_bytes=64)
-        w_raw = [keep.tile([P, 4, H // 2], F32, name=f"w_raw{a}", tag=f"w_raw{a}", align_bytes=64) for a in range(2)]
+        w_pieces = [(0, W_SPLIT), (W_SPLIT, P)]
+        w_raw = [keep.tile([P, 4, 4 * (m1 - m0)], F32, name=f"w_raw{a}", align_bytes=64) for a, (m0, m1) in enumerate(w_pieces)]
         gain_sb = keep.tile([P, V], F32, name="gain_sb")
+        xs = keep.tile([P, S], U8, name="xs", align_bytes=64)
+        ns = keep.tile([P, D, V], U8, name="ns", align_bytes=64)
+        ps = keep.tile([P, V], U8, name="ps", align_bytes=64)
 
-        nc.vector.memset(es_all[:].bitcast(I32), 0)
-        nc.gpsimd.memset(xs_all[:].bitcast(I32), 0)
-
-        def load_scale_rows(plane, rows, q):
-            nc.sync.dma_start(plane[q:P:32, :].bitcast(I32), rows[0, q:16:4, :].bitcast(I32))
+        nc.vector.memset(xs_all[0:ROW0, :].bitcast(I32), 0)
+        nc.vector.memset(es_all[0:ROW0, :].bitcast(I32), 0)
+        nc.vector.memset(xs[:].bitcast(I32), 0)
+        nc.vector.memset(ps[:].bitcast(I32), 0)
+        nc.vector.memset(ns[:].rearrange("p d v -> p (d v)").bitcast(I32), 0)
 
         w_view = w1.rearrange("(p j) c -> p j c", j=4)
-        nc.sync.dma_start(neg_sb[:], neg)
-        nc.sync.dma_start(w_raw[0][:], w_view[:, :, 0 : H // 2])
-        nc.sync.dma_start(pos_sb[:], pos)
-        for q in range(4):
-            load_scale_rows(es_all, e_scales, q)
-        nc.sync.dma_start(w_raw[1][:], w_view[:, :, H // 2 : H])
-        nc.sync.dma_start(xw_all[:], x_words[0].rearrange("p n t -> p (n t)").bitcast(I32))
-        for q in range(4):
-            load_scale_rows(xs_all, x_scales, q)
-        nc.sync.dma_start(offs_sb[:], offs)
-        nc.sync.dma_start(ew_all[:], e_words[0].rearrange("p n t -> p (n t)").bitcast(I32))
-        nc.sync.dma_start(gain_sb[:], gain)
 
-        xs = keep.tile([P, S], U8, name="xs", align_bytes=64)
-        ns_listed = keep.tile([P, U], U8, name="ns_listed", align_bytes=64)
-        ps = keep.tile([P, V], U8, name="ps", align_bytes=64)
+        def load_w(a):
+            m0, m1 = w_pieces[a]
+            nc.sync.dma_start(w_raw[a][:], w_view[:, :, 4 * m0 : 4 * m1])
+
+        nc.sync.dma_start(offs_sb[:], offs)
+        nc.sync.dma_start(xs_all[ROW0:P, :].bitcast(I32), x_scales[0].bitcast(I32))
+        load_w(0)
+        nc.sync.dma_start(neg_sb[:], neg)
+        nc.sync.dma_start(pos_sb[:], pos)
+        nc.sync.dma_start(es_all[ROW0:P, :].bitcast(I32), e_scales[0].bitcast(I32))
+        load_w(1)
+        nc.sync.dma_start(xw_all[:], x_words[0].rearrange("p n t -> p (n t)").bitcast(I32))
+        nc.sync.dma_start(ew_all[:], e_words[0].rearrange("p n t -> p (n t)").bitcast(I32))
+
+        def place_rows(plane, picked):
+            for q in range(4):
+                nc.sync.dma_start(plane[32 * q : 32 * q + 4, :].bitcast(I32), picked[ROW0 + 4 * q : ROW0 + 4 * q + 4, :].bitcast(I32))
+
+        xs_picked = keep.tile([P, S], U8, name="xs_picked", align_bytes=64)
+        ns_picked = keep.tile([P, U], U8, name="ns_picked", align_bytes=64)
+        ps_picked = keep.tile([P, V], U8, name="ps_picked", align_bytes=64)
+        ns_parted = keep.tile([P, D, V], U8, name="ns_parted", align_bytes=64)
         xw = keep.tile([P, S], U32, name="xw", align_bytes=64)
         pw = keep.tile([P, V], U32, name="pw", align_bytes=64)
         nw = keep.tile([P, D, V], U32, name="nw", align_bytes=64)
 
-        ns = keep.tile([P, D, V], U8, name="ns", align_bytes=64)
-        nc.vector.tensor_copy(ns_listed[:], es_all[:].indirect(neg_sb[:]))
-        nc.vector.tensor_copy(ps[:], es_all[:].indirect(pos_sb[:]))
-        nc.vector.tensor_copy(ns[:], ns_listed[:].rearrange("p (v d) -> p d v", d=D))
+        nc.vector.tensor_copy(xs_picked[:], xs_all[:].indirect(offs_sb[:]))
+        nc.vector.tensor_copy(ns_picked[:], es_all[:].indirect(neg_sb[:]))
+        nc.vector.tensor_copy(ps_picked[:], es_all[:].indirect(pos_sb[:]))
+        nc.vector.tensor_copy(ns_parted[:], ns_picked[:].rearrange("p (v d) -> p d v", d=D))
+        place_rows(xs, xs_picked)
+        place_rows(ps, ps_picked)
+        place_rows(ns[:].rearrange("p d v -> p (d v)"), ns_parted[:].rearrange("p d v -> p (d v)"))
+        nc.sync.dma_start(gain_sb[:], gain)
 
-        w_bf = [keep.tile([P, 4, 64, 4], BF16, name=f"w_bf{a}", align_bytes=64) for a in range(2)]
-
-        def cast_views(m0, m1):
-            a = m0 // 64
-            return (
-                w_bf[a][:, :, m0 - 64 * a : m1 - 64 * a, :].rearrange("p t m j -> p m j t"),
-                w_raw[a][:, :, 4 * (m0 - 64 * a) : 4 * (m1 - 64 * a)].rearrange("p j (m t) -> p m j t", t=4),
+        w_bf = keep.tile([P, 4, P, 4], BF16, name="w_bf", align_bytes=64)
+        for a, (m0, m1) in enumerate(w_pieces):
+            nc.scalar.activation(
+                w_bf[:, :, m0:m1, :].rearrange("p t m j -> p m j t"),
+                w_raw[a][:].rearrange("p j (m t) -> p m j t", t=4),
+                ACT.Copy,
             )
 
-        nc.vector.tensor_copy(*cast_views(48, 64))
-        nc.scalar.activation(*cast_views(0, 48), ACT.Copy)
-        nc.scalar.activation(*cast_views(64, P), ACT.Copy)
-        wq = keep.tile([P, H], U32, name="wq", tag="es_then_wq", align_bytes=64)
-        wq_s = keep.tile([P, H], U8, name="wq_s", align_bytes=64)
-        for a in range(2):
-            for t in range(4):
-                cols = slice(P * t + 64 * a, P * t + 64 * (a + 1))
-                nc.vector.quantize_mx(out=wq[:, cols].bitcast(FP8X4), scales=wq_s[:, cols], in_=w_bf[a][:, t, :, :].rearrange("p m j -> p (m j)"))
-        for c0, c1 in [(0, S // 2), (S // 2, S)]:
+        def gather_x_words(c0, c1):
             nc.vector.tensor_copy(xw[:, c0:c1], xw_all[:].bitcast(U32).indirect(offs_sb[:, c0 // 16 : c1 // 16]))
-            nc.vector.tensor_copy(xs[:, c0:c1], xs_all[:].indirect(offs_sb[:, c0 // 16 : c1 // 16]))
+
+        gather_x_words(0, S // 2)
+        wq = keep.tile([P, H], U32, name="wq", align_bytes=64)
+        wq_s = keep.tile([P, H], U8, name="wq_s", align_bytes=64)
+        for t in range(4):
+            cols = slice(P * t, P * (t + 1))
+            nc.vector.quantize_mx(out=wq[:, cols].bitcast(FP8X4), scales=wq_s[:, cols], in_=w_bf[:, t, :, :].rearrange("p m j -> p (m j)"))
+        gather_x_words(S // 2, S)
 
         h_bf = []
-        minus = []
+        minus_h = []
         for i in range(TILES):
             h_ps = psum.tile([P, 4, P], F32, name="h_ps", tag="bank", bufs=8)
             for t in range(4):
@@ -105,39 +120,36 @@ def tile_picked_ysmap_log_p_kernel(
                     start=True,
                     stop=True,
                 )
-            hb = keep.tile([P, P, 4], BF16, name=f"h_bf{i}", align_bytes=64)
-            nc.scalar.activation(hb[:], h_ps[:].rearrange("p t n -> p n t"), ACT.Copy)
-            h_bf.append(hb)
-            minus.append(keep.tile([P, P, 4], BF16, name=f"minus_h{i}", align_bytes=64))
+            h_bf.append(keep.tile([P, P, 4], BF16, name=f"h_bf{i}", align_bytes=64))
+            minus_h.append(keep.tile([P, P, 4], BF16, name=f"minus_h{i}", align_bytes=64))
+            nc.scalar.activation(h_bf[i][:], h_ps[:].rearrange("p t n -> p n t"), ACT.Copy)
             if i < SCALAR_NEGATES:
-                nc.scalar.activation(minus[i][:], h_ps[:].rearrange("p t n -> p n t"), ACT.Copy, scale=-1.0)
+                nc.scalar.activation(minus_h[i][:], h_ps[:].rearrange("p t n -> p n t"), ACT.Copy, scale=-1.0)
 
         nc.vector.tensor_copy(pw[:], ew_all[:].bitcast(U32).indirect(pos_sb[:]))
         nc.vector.tensor_copy(nw[:].rearrange("p d v -> p v d"), ew_all[:].bitcast(U32).indirect(neg_sb[:]))
 
-        def quantize(name, codes, values):
+        def quantize(name, values):
+            codes = keep.tile([P, P], U32, name=name, align_bytes=64)
             scales = keep.tile([P, P], U8, name=name + "_s", align_bytes=64)
             nc.vector.quantize_mx(out=codes[:].bitcast(FP8X4), scales=scales[:], in_=values[:].rearrange("p n t -> p (n t)"))
-            return scales
+            return codes, scales
 
         th = keep.tile([P, TILES, D, V], F32, name="th")
         for i in range(TILES):
-            minus_h = minus[i]
-            mq = keep.tile([P, P], U32, name=f"mq{i}", align_bytes=64)
             if i >= SCALAR_NEGATES:
-                nc.vector.tensor_scalar(minus_h[:], h_bf[i][:], -1.0, None, ALU.mult)
-            hq = keep.tile([P, P], U32, name=f"hq{i}", align_bytes=64)
-            hq_s = quantize(f"hq{i}", hq, h_bf[i])
-            mq_s = quantize(f"mq{i}", mq, minus_h)
+                nc.vector.tensor_scalar(minus_h[i][:], h_bf[i][:], -1.0, None, ALU.mult)
+            hq, hq_s = quantize(f"hq{i}", h_bf[i])
+            mq, mq_s = quantize(f"mq{i}", minus_h[i])
             for members in ([(0,), (1,)] if i in (0, TILES - 1) else [(0, 1)]):
-              z_ps = psum.tile([P, D, V], F32, name="z_ps", tag="bank", bufs=8)
-              for d in members:
-                nc.tensor.matmul_mx(out=z_ps[:, d, :], lhsT=hq[:].bitcast(FP8X4), lhsT_scale=hq_s[:],
-                                    rhs=nw[:, d, :].bitcast(FP8X4), rhs_scale=ns[:, d, :], start=True, stop=False)
-                nc.tensor.matmul_mx(out=z_ps[:, d, :], lhsT=mq[:].bitcast(FP8X4), lhsT_scale=mq_s[:],
-                                    rhs=pw[:].bitcast(FP8X4), rhs_scale=ps[:], start=False, stop=True)
-              ds = slice(members[0], members[-1] + 1)
-              nc.scalar.activation(th[:, i, ds, :], z_ps[:, ds, :], ACT.Tanh, scale=2.0)
+                z_ps = psum.tile([P, D, V], F32, name="z_ps", tag="bank", bufs=8)
+                for d in members:
+                    nc.tensor.matmul_mx(out=z_ps[:, d, :], lhsT=hq[:].bitcast(FP8X4), lhsT_scale=hq_s[:],
+                                        rhs=nw[:, d, :].bitcast(FP8X4), rhs_scale=ns[:, d, :], start=True, stop=False)
+                    nc.tensor.matmul_mx(out=z_ps[:, d, :], lhsT=mq[:].bitcast(FP8X4), lhsT_scale=mq_s[:],
+                                        rhs=pw[:].bitcast(FP8X4), rhs_scale=ps[:], start=False, stop=True)
+                ds = slice(members[0], members[-1] + 1)
+                nc.scalar.activation(th[:, i, ds, :], z_ps[:, ds, :], ACT.Tanh, scale=2.0)
 
         sums = keep.tile([P, TILES, V], F32, name="sums")
         nc.vector.tensor_tensor(sums[:], th[:, :, 0, :], th[:, :, 1, :], ALU.add)

@@ -18,7 +18,8 @@ TILES = S // P
 ROWS = 16
 ROW0 = P - ROWS
 W_SPLIT = 48
-SCALAR_NEGATES = 1
+SCALAR_NEGATES = 0
+HALF_PLACED = 4096
 FLOPS = 2 * K * H * S + 2 * H * S * U + 2 * H * S * V
 
 
@@ -28,6 +29,7 @@ def tile_picked_ysmap_log_p_kernel(
     nc = tc.nc
     with ExitStack() as ctx:
         keep = ctx.enter_context(tc.tile_pool(name="keep", bufs=1))
+        placed = ctx.enter_context(tc.tile_pool(name="placed", bufs=1))
         psum = ctx.enter_context(tc.psum_pool(name="psum", bufs=1))
 
         offs_sb = keep.tile([P, S // 16], U16, name="offs_sb")
@@ -38,17 +40,15 @@ def tile_picked_ysmap_log_p_kernel(
         xw_all = keep.tile([P, T], I32, name="xw_all", align_bytes=64)
         ew_all = keep.tile([P, W], I32, name="ew_all", align_bytes=64)
         w_pieces = [(0, W_SPLIT), (W_SPLIT, P)]
-        w_raw = [keep.tile([P, 4, 4 * (m1 - m0)], F32, name=f"w_raw{a}", align_bytes=64) for a, (m0, m1) in enumerate(w_pieces)]
+        w_raw = [keep.tile([P, 4, 4 * (m1 - m0)], F32, name=f"w_raw{a}", tag=f"w_raw{a}", align_bytes=64) for a, (m0, m1) in enumerate(w_pieces)]
         gain_sb = keep.tile([P, V], F32, name="gain_sb")
         xs = keep.tile([P, S], U8, name="xs", align_bytes=64)
-        ns = keep.tile([P, D, V], U8, name="ns", align_bytes=64)
-        ps = keep.tile([P, V], U8, name="ps", align_bytes=64)
+        es = keep.tile([P, (D + 1) * V], U8, name="es", align_bytes=64)
 
         nc.vector.memset(xs_all[0:ROW0, :].bitcast(I32), 0)
         nc.vector.memset(es_all[0:ROW0, :].bitcast(I32), 0)
         nc.vector.memset(xs[:].bitcast(I32), 0)
-        nc.vector.memset(ps[:].bitcast(I32), 0)
-        nc.vector.memset(ns[:].rearrange("p d v -> p (d v)").bitcast(I32), 0)
+        nc.vector.memset(es[:].bitcast(I32), 0)
 
         w_view = w1.rearrange("(p j) c -> p j c", j=4)
 
@@ -64,7 +64,6 @@ def tile_picked_ysmap_log_p_kernel(
         nc.sync.dma_start(es_all[ROW0:P, :].bitcast(I32), e_scales[0].bitcast(I32))
         load_w(1)
         nc.sync.dma_start(xw_all[:], x_words[0].rearrange("p n t -> p (n t)").bitcast(I32))
-        nc.sync.dma_start(ew_all[:], e_words[0].rearrange("p n t -> p (n t)").bitcast(I32))
 
         def place_rows(plane, picked):
             for q in range(4):
@@ -73,18 +72,18 @@ def tile_picked_ysmap_log_p_kernel(
         xs_picked = keep.tile([P, S], U8, name="xs_picked", align_bytes=64)
         ns_picked = keep.tile([P, U], U8, name="ns_picked", align_bytes=64)
         ps_picked = keep.tile([P, V], U8, name="ps_picked", align_bytes=64)
-        ns_parted = keep.tile([P, D, V], U8, name="ns_parted", align_bytes=64)
-        xw = keep.tile([P, S], U32, name="xw", align_bytes=64)
+        es_dealt = placed.tile([P, (D + 1) * V], U8, name="es_dealt", offset=HALF_PLACED - 384, align_bytes=64)
         pw = keep.tile([P, V], U32, name="pw", align_bytes=64)
         nw = keep.tile([P, D, V], U32, name="nw", align_bytes=64)
 
         nc.vector.tensor_copy(xs_picked[:], xs_all[:].indirect(offs_sb[:]))
         nc.vector.tensor_copy(ns_picked[:], es_all[:].indirect(neg_sb[:]))
         nc.vector.tensor_copy(ps_picked[:], es_all[:].indirect(pos_sb[:]))
-        nc.vector.tensor_copy(ns_parted[:], ns_picked[:].rearrange("p (v d) -> p d v", d=D))
+        nc.vector.tensor_copy(es_dealt[:, 0:U].rearrange("p (d v) -> p v d", d=D), ns_picked[:].rearrange("p (v d) -> p v d", d=D))
+        nc.vector.tensor_copy(es_dealt[:, U : U + V].bitcast(I32), ps_picked[:].bitcast(I32))
         place_rows(xs, xs_picked)
-        place_rows(ps, ps_picked)
-        place_rows(ns[:].rearrange("p d v -> p (d v)"), ns_parted[:].rearrange("p d v -> p (d v)"))
+        nc.sync.dma_start(ew_all[:], e_words[0].rearrange("p n t -> p (n t)").bitcast(I32))
+        place_rows(es, es_dealt)
         nc.sync.dma_start(gain_sb[:], gain)
 
         w_bf = keep.tile([P, 4, P, 4], BF16, name="w_bf", align_bytes=64)
@@ -95,19 +94,23 @@ def tile_picked_ysmap_log_p_kernel(
                 ACT.Copy,
             )
 
-        def gather_x_words(c0, c1):
-            nc.vector.tensor_copy(xw[:, c0:c1], xw_all[:].bitcast(U32).indirect(offs_sb[:, c0 // 16 : c1 // 16]))
+        def gather_x_words(half, tag):
+            picked = keep.tile([P, S // 2], U32, name=f"xw{half}", tag=tag, align_bytes=64)
+            nc.vector.tensor_copy(picked[:], xw_all[:].bitcast(U32).indirect(offs_sb[:, 16 * half : 16 * (half + 1)]))
+            return picked
 
-        gather_x_words(0, S // 2)
+        xw = [gather_x_words(0, "xw0")]
         wq = keep.tile([P, H], U32, name="wq", align_bytes=64)
         wq_s = keep.tile([P, H], U8, name="wq_s", align_bytes=64)
         for t in range(4):
             cols = slice(P * t, P * (t + 1))
             nc.vector.quantize_mx(out=wq[:, cols].bitcast(FP8X4), scales=wq_s[:, cols], in_=w_bf[:, t, :, :].rearrange("p m j -> p (m j)"))
-        gather_x_words(S // 2, S)
+        xw.append(gather_x_words(1, "w_raw1"))
 
         h_bf = []
-        minus_h = []
+        minus_all = placed.tile([P, TILES * 4 * P], BF16, name="minus_all", offset=0, align_bytes=64)
+        codes_all = placed.tile([P, 2 * TILES * P], U32, name="codes_all", offset=HALF_PLACED, align_bytes=64)
+        minus_h = [minus_all[:, 4 * P * i : 4 * P * (i + 1)] for i in range(TILES)]
         for i in range(TILES):
             h_ps = psum.tile([P, 4, P], F32, name="h_ps", tag="bank", bufs=8)
             for t in range(4):
@@ -115,39 +118,38 @@ def tile_picked_ysmap_log_p_kernel(
                     out=h_ps[:, t, :],
                     lhsT=wq[:, P * t : P * (t + 1)].bitcast(FP8X4),
                     lhsT_scale=wq_s[:, P * t : P * (t + 1)],
-                    rhs=xw[:, P * i : P * (i + 1)].bitcast(FP8X4),
+                    rhs=xw[i // 2][:, P * (i % 2) : P * (i % 2 + 1)].bitcast(FP8X4),
                     rhs_scale=xs[:, P * i : P * (i + 1)],
                     start=True,
                     stop=True,
                 )
             h_bf.append(keep.tile([P, P, 4], BF16, name=f"h_bf{i}", align_bytes=64))
-            minus_h.append(keep.tile([P, P, 4], BF16, name=f"minus_h{i}", align_bytes=64))
             nc.scalar.activation(h_bf[i][:], h_ps[:].rearrange("p t n -> p n t"), ACT.Copy)
             if i < SCALAR_NEGATES:
-                nc.scalar.activation(minus_h[i][:], h_ps[:].rearrange("p t n -> p n t"), ACT.Copy, scale=-1.0)
+                nc.scalar.activation(minus_h[i].rearrange("p (n t) -> p n t", t=4), h_ps[:].rearrange("p t n -> p n t"), ACT.Copy, scale=-1.0)
 
         nc.vector.tensor_copy(pw[:], ew_all[:].bitcast(U32).indirect(pos_sb[:]))
         nc.vector.tensor_copy(nw[:].rearrange("p d v -> p v d"), ew_all[:].bitcast(U32).indirect(neg_sb[:]))
 
-        def quantize(name, values):
-            codes = keep.tile([P, P], U32, name=name, align_bytes=64)
-            scales = keep.tile([P, P], U8, name=name + "_s", align_bytes=64)
-            nc.vector.quantize_mx(out=codes[:].bitcast(FP8X4), scales=scales[:], in_=values[:].rearrange("p n t -> p (n t)"))
+        def quantize(k, values):
+            codes = codes_all[:, P * k : P * (k + 1)]
+            scales = keep.tile([P, P], U8, name=f"h_scales{k}", align_bytes=64)
+            nc.vector.quantize_mx(out=codes.bitcast(FP8X4), scales=scales[:], in_=values)
             return codes, scales
 
         th = keep.tile([P, TILES, D, V], F32, name="th")
         for i in range(TILES):
             if i >= SCALAR_NEGATES:
-                nc.vector.tensor_scalar(minus_h[i][:], h_bf[i][:], -1.0, None, ALU.mult)
-            hq, hq_s = quantize(f"hq{i}", h_bf[i])
-            mq, mq_s = quantize(f"mq{i}", minus_h[i])
+                nc.vector.tensor_scalar(minus_h[i], h_bf[i][:].rearrange("p n t -> p (n t)"), -1.0, None, ALU.mult)
+            hq, hq_s = quantize(2 * i, h_bf[i][:].rearrange("p n t -> p (n t)"))
+            mq, mq_s = quantize(2 * i + 1, minus_h[i])
             for members in ([(0,), (1,)] if i in (0, TILES - 1) else [(0, 1)]):
                 z_ps = psum.tile([P, D, V], F32, name="z_ps", tag="bank", bufs=8)
                 for d in members:
-                    nc.tensor.matmul_mx(out=z_ps[:, d, :], lhsT=hq[:].bitcast(FP8X4), lhsT_scale=hq_s[:],
-                                        rhs=nw[:, d, :].bitcast(FP8X4), rhs_scale=ns[:, d, :], start=True, stop=False)
-                    nc.tensor.matmul_mx(out=z_ps[:, d, :], lhsT=mq[:].bitcast(FP8X4), lhsT_scale=mq_s[:],
-                                        rhs=pw[:].bitcast(FP8X4), rhs_scale=ps[:], start=False, stop=True)
+                    nc.tensor.matmul_mx(out=z_ps[:, d, :], lhsT=hq.bitcast(FP8X4), lhsT_scale=hq_s[:],
+                                        rhs=nw[:, d, :].bitcast(FP8X4), rhs_scale=es[:, V * d : V * (d + 1)], start=True, stop=False)
+                    nc.tensor.matmul_mx(out=z_ps[:, d, :], lhsT=mq.bitcast(FP8X4), lhsT_scale=mq_s[:],
+                                        rhs=pw[:].bitcast(FP8X4), rhs_scale=es[:, U : U + V], start=False, stop=True)
                 ds = slice(members[0], members[-1] + 1)
                 nc.scalar.activation(th[:, i, ds, :], z_ps[:, ds, :], ACT.Tanh, scale=2.0)
 

@@ -17,8 +17,9 @@ K, T, S, H, D, V, W, U = 512, 1024, 512, 512, 2, 256, 1024, 512
 TILES = S // P
 ROWS = 16
 ROW0 = P - ROWS
-W_SPLIT = 48
+W_CUTS = (0, 64, 96, 128)
 SCALAR_NEGATES = 0
+X_EARLY = 4
 HALF_PLACED = 4096
 FLOPS = 2 * K * H * S + 2 * H * S * U + 2 * H * S * V
 
@@ -39,7 +40,7 @@ def tile_picked_ysmap_log_p_kernel(
         es_all = keep.tile([P, W], U8, name="es_all", align_bytes=64)
         xw_all = keep.tile([P, T], I32, name="xw_all", align_bytes=64)
         ew_all = keep.tile([P, W], I32, name="ew_all", align_bytes=64)
-        w_pieces = [(0, W_SPLIT), (W_SPLIT, P)]
+        w_pieces = list(zip(W_CUTS, W_CUTS[1:]))
         w_raw = [keep.tile([P, 4, 4 * (m1 - m0)], F32, name=f"w_raw{a}", tag=f"w_raw{a}", align_bytes=64) for a, (m0, m1) in enumerate(w_pieces)]
         gain_sb = keep.tile([P, V], F32, name="gain_sb")
         xs = keep.tile([P, S], U8, name="xs", align_bytes=64)
@@ -57,30 +58,27 @@ def tile_picked_ysmap_log_p_kernel(
             nc.sync.dma_start(w_raw[a][:], w_view[:, :, 4 * m0 : 4 * m1])
 
         nc.sync.dma_start(offs_sb[:], offs)
-        nc.sync.dma_start(xs_all[ROW0:P, :].bitcast(I32), x_scales[0].bitcast(I32))
+        nc.scalar.dma_start(xs_all[ROW0:P, :].bitcast(I32), x_scales[0].bitcast(I32))
         load_w(0)
         nc.sync.dma_start(neg_sb[:], neg)
-        nc.sync.dma_start(pos_sb[:], pos)
         nc.sync.dma_start(es_all[ROW0:P, :].bitcast(I32), e_scales[0].bitcast(I32))
         load_w(1)
+        nc.sync.dma_start(pos_sb[:], pos)
         nc.sync.dma_start(xw_all[:], x_words[0].rearrange("p n t -> p (n t)").bitcast(I32))
+        load_w(2)
 
         def place_rows(plane, picked):
             for q in range(4):
                 nc.sync.dma_start(plane[32 * q : 32 * q + 4, :].bitcast(I32), picked[ROW0 + 4 * q : ROW0 + 4 * q + 4, :].bitcast(I32))
 
         xs_picked = keep.tile([P, S], U8, name="xs_picked", align_bytes=64)
-        ns_picked = keep.tile([P, U], U8, name="ns_picked", align_bytes=64)
-        ps_picked = keep.tile([P, V], U8, name="ps_picked", align_bytes=64)
         es_dealt = placed.tile([P, (D + 1) * V], U8, name="es_dealt", offset=HALF_PLACED - 384, align_bytes=64)
         pw = keep.tile([P, V], U32, name="pw", align_bytes=64)
         nw = keep.tile([P, D, V], U32, name="nw", align_bytes=64)
 
         nc.vector.tensor_copy(xs_picked[:], xs_all[:].indirect(offs_sb[:]))
-        nc.vector.tensor_copy(ns_picked[:], es_all[:].indirect(neg_sb[:]))
-        nc.vector.tensor_copy(ps_picked[:], es_all[:].indirect(pos_sb[:]))
-        nc.vector.tensor_copy(es_dealt[:, 0:U].rearrange("p (d v) -> p v d", d=D), ns_picked[:].rearrange("p (v d) -> p v d", d=D))
-        nc.vector.tensor_copy(es_dealt[:, U : U + V].bitcast(I32), ps_picked[:].bitcast(I32))
+        nc.vector.tensor_copy(es_dealt[:, 0:U].rearrange("p (d v) -> p v d", d=D), es_all[:].indirect(neg_sb[:]))
+        nc.vector.tensor_copy(es_dealt[:, U : U + V], es_all[:].indirect(pos_sb[:]))
         place_rows(xs, xs_picked)
         nc.sync.dma_start(ew_all[:], e_words[0].rearrange("p n t -> p (n t)").bitcast(I32))
         place_rows(es, es_dealt)
@@ -94,18 +92,18 @@ def tile_picked_ysmap_log_p_kernel(
                 ACT.Copy,
             )
 
-        def gather_x_words(half, tag):
-            picked = keep.tile([P, S // 2], U32, name=f"xw{half}", tag=tag, align_bytes=64)
-            nc.vector.tensor_copy(picked[:], xw_all[:].bitcast(U32).indirect(offs_sb[:, 16 * half : 16 * (half + 1)]))
-            return picked
+        def gather_x_words(t0, t1, tag):
+            picked = keep.tile([P, P * (t1 - t0)], U32, name=f"xw{t0}", tag=tag, align_bytes=64)
+            nc.vector.tensor_copy(picked[:], xw_all[:].bitcast(U32).indirect(offs_sb[:, 8 * t0 : 8 * t1]))
+            return [picked[:, P * i : P * (i + 1)] for i in range(t1 - t0)]
 
-        xw = [gather_x_words(0, "xw0")]
+        xw = gather_x_words(0, X_EARLY, "xw0")
         wq = keep.tile([P, H], U32, name="wq", align_bytes=64)
         wq_s = keep.tile([P, H], U8, name="wq_s", align_bytes=64)
         for t in range(4):
             cols = slice(P * t, P * (t + 1))
             nc.vector.quantize_mx(out=wq[:, cols].bitcast(FP8X4), scales=wq_s[:, cols], in_=w_bf[:, t, :, :].rearrange("p m j -> p (m j)"))
-        xw.append(gather_x_words(1, "w_raw1"))
+
 
         h_bf = []
         minus_all = placed.tile([P, TILES * 4 * P], BF16, name="minus_all", offset=0, align_bytes=64)
@@ -118,7 +116,7 @@ def tile_picked_ysmap_log_p_kernel(
                     out=h_ps[:, t, :],
                     lhsT=wq[:, P * t : P * (t + 1)].bitcast(FP8X4),
                     lhsT_scale=wq_s[:, P * t : P * (t + 1)],
-                    rhs=xw[i // 2][:, P * (i % 2) : P * (i % 2 + 1)].bitcast(FP8X4),
+                    rhs=xw[i].bitcast(FP8X4),
                     rhs_scale=xs[:, P * i : P * (i + 1)],
                     start=True,
                     stop=True,
@@ -158,9 +156,12 @@ def tile_picked_ysmap_log_p_kernel(
 
         HALF = V // 2
         for i in range(TILES):
+            res = keep.tile([P, V], F32, name=f"res{i}")
             for c0, c1 in ([(0, HALF), (HALF, V)] if i in (0, TILES - 1) else [(0, V)]):
                 lg = keep.tile([P, c1 - c0], F32, name=f"lg{i}_{c0}")
                 nc.scalar.activation(lg[:], sums[:, i, c0:c1], ACT.Ln, scale=0.5, bias=2.0)
-                res = keep.tile([P, c1 - c0], F32, name=f"res{i}_{c0}")
-                nc.vector.tensor_tensor(res[:], lg[:], gain_sb[:, c0:c1], ALU.mult)
-                nc.sync.dma_start(out[P * i : P * (i + 1), c0:c1], res[:])
+                nc.vector.tensor_tensor(res[:, c0:c1], lg[:], gain_sb[:, c0:c1], ALU.mult)
+                if i == TILES - 1:
+                    nc.sync.dma_start(out[P * i : P * (i + 1), c0:c1], res[:, c0:c1])
+            if i < TILES - 1:
+                nc.sync.dma_start(out[P * i : P * (i + 1), :], res[:])

@@ -17,9 +17,9 @@ K, T, S, H, D, V, W, U = 512, 1024, 512, 512, 2, 256, 1024, 512
 TILES = S // P
 ROWS = 16
 ROW0 = P - ROWS
-W_CUTS = (0, 64, 96, 128)
+W_CUTS = (0, 48, 96, 128)
 SCALAR_NEGATES = 0
-X_EARLY = 4
+X_EARLY = 3
 HALF_PLACED = 4096
 FLOPS = 2 * K * H * S + 2 * H * S * U + 2 * H * S * V
 
@@ -86,11 +86,12 @@ def tile_picked_ysmap_log_p_kernel(
 
         w_bf = keep.tile([P, 4, P, 4], BF16, name="w_bf", align_bytes=64)
         for a, (m0, m1) in enumerate(w_pieces):
-            nc.scalar.activation(
-                w_bf[:, :, m0:m1, :].rearrange("p t m j -> p m j t"),
-                w_raw[a][:].rearrange("p j (m t) -> p m j t", t=4),
-                ACT.Copy,
-            )
+            for t0, t1 in ([(0, 2), (2, 4)] if m1 == P else [(0, 4)]):
+                nc.scalar.activation(
+                    w_bf[:, t0:t1, m0:m1, :].rearrange("p t m j -> p m j t"),
+                    w_raw[a][:].rearrange("p j (m t) -> p m j t", t=4)[:, :, :, t0:t1],
+                    ACT.Copy,
+                )
 
         def gather_x_words(t0, t1, tag):
             picked = keep.tile([P, P * (t1 - t0)], U32, name=f"xw{t0}", tag=tag, align_bytes=64)
@@ -104,6 +105,8 @@ def tile_picked_ysmap_log_p_kernel(
             cols = slice(P * t, P * (t + 1))
             nc.vector.quantize_mx(out=wq[:, cols].bitcast(FP8X4), scales=wq_s[:, cols], in_=w_bf[:, t, :, :].rearrange("p m j -> p (m j)"))
 
+
+        xw.extend(gather_x_words(X_EARLY, TILES, "w_raw2"))
 
         h_bf = []
         minus_all = placed.tile([P, TILES * 4 * P], BF16, name="minus_all", offset=0, align_bytes=64)
@@ -141,7 +144,7 @@ def tile_picked_ysmap_log_p_kernel(
                 nc.vector.tensor_scalar(minus_h[i], h_bf[i][:].rearrange("p n t -> p (n t)"), -1.0, None, ALU.mult)
             hq, hq_s = quantize(2 * i, h_bf[i][:].rearrange("p n t -> p (n t)"))
             mq, mq_s = quantize(2 * i + 1, minus_h[i])
-            for members in ([(0,), (1,)] if i in (0, TILES - 1) else [(0, 1)]):
+            for members in [(0,), (1,)]:
                 z_ps = psum.tile([P, D, V], F32, name="z_ps", tag="bank", bufs=8)
                 for d in members:
                     nc.tensor.matmul_mx(out=z_ps[:, d, :], lhsT=hq.bitcast(FP8X4), lhsT_scale=hq_s[:],

@@ -17,7 +17,7 @@ K, T, S, H, D, V, W, U = 512, 1024, 512, 512, 2, 256, 1024, 512
 TILES = S // P
 ROWS = 16
 ROW0 = P - ROWS
-W_CUTS = (0, 48, 96, 128)
+W_PIECES = ((0, 2, 0, 96), (2, 4, 0, 96), (0, 4, 96, 128))
 SCALAR_NEGATES = 0
 X_EARLY = 3
 HALF_PLACED = 4096
@@ -40,8 +40,7 @@ def tile_picked_ysmap_log_p_kernel(
         es_all = keep.tile([P, W], U8, name="es_all", align_bytes=64)
         xw_all = keep.tile([P, T], I32, name="xw_all", align_bytes=64)
         ew_all = keep.tile([P, W], I32, name="ew_all", align_bytes=64)
-        w_pieces = list(zip(W_CUTS, W_CUTS[1:]))
-        w_raw = [keep.tile([P, 4, 4 * (m1 - m0)], F32, name=f"w_raw{a}", tag=f"w_raw{a}", align_bytes=64) for a, (m0, m1) in enumerate(w_pieces)]
+        w_raw = [keep.tile([P, j1 - j0, 4 * (m1 - m0)], F32, name=f"w_raw{a}", tag=f"w_raw{a}", align_bytes=64) for a, (j0, j1, m0, m1) in enumerate(W_PIECES)]
         gain_sb = keep.tile([P, V], F32, name="gain_sb")
         xs = keep.tile([P, S], U8, name="xs", align_bytes=64)
         es = keep.tile([P, (D + 1) * V], U8, name="es", align_bytes=64)
@@ -54,8 +53,8 @@ def tile_picked_ysmap_log_p_kernel(
         w_view = w1.rearrange("(p j) c -> p j c", j=4)
 
         def load_w(a):
-            m0, m1 = w_pieces[a]
-            nc.sync.dma_start(w_raw[a][:], w_view[:, :, 4 * m0 : 4 * m1])
+            j0, j1, m0, m1 = W_PIECES[a]
+            nc.sync.dma_start(w_raw[a][:], w_view[:, j0:j1, 4 * m0 : 4 * m1])
 
         nc.sync.dma_start(offs_sb[:], offs)
         nc.scalar.dma_start(xs_all[ROW0:P, :].bitcast(I32), x_scales[0].bitcast(I32))
@@ -85,10 +84,10 @@ def tile_picked_ysmap_log_p_kernel(
         nc.sync.dma_start(gain_sb[:], gain)
 
         w_bf = keep.tile([P, 4, P, 4], BF16, name="w_bf", align_bytes=64)
-        for a, (m0, m1) in enumerate(w_pieces):
-            for t0, t1 in ([(0, 2), (2, 4)] if m1 == P else [(0, 4)]):
+        for a, (j0, j1, m0, m1) in enumerate(W_PIECES):
+            for t0, t1 in ([(0, 2), (2, 4)] if a == len(W_PIECES) - 1 else [(0, 4)]):
                 nc.scalar.activation(
-                    w_bf[:, t0:t1, m0:m1, :].rearrange("p t m j -> p m j t"),
+                    w_bf[:, t0:t1, m0:m1, j0:j1].rearrange("p t m j -> p m j t"),
                     w_raw[a][:].rearrange("p j (m t) -> p m j t", t=4)[:, :, :, t0:t1],
                     ACT.Copy,
                 )

from contextlib import ExitStack

import concourse.mybir as mybir

F32 = mybir.dt.float32
BF16 = mybir.dt.bfloat16
I32 = mybir.dt.int32
U32 = mybir.dt.uint32
U16 = mybir.dt.uint16
U8 = mybir.dt.uint8
FP8X4 = mybir.dt.float8_e4m3fn_x4
ACT = mybir.ActivationFunctionType
ALU = mybir.AluOpType

P = 128
K, T, S, H, D, V, W, U = 512, 1024, 512, 512, 2, 256, 1024, 512
TILES = S // P
ROWS = 16
ROW0 = P - ROWS
W_PIECES = ((0, 2, 0, 96), (2, 4, 0, 96), (0, 4, 96, 128))
SCALAR_NEGATES = 0
X_EARLY = 3
HALF_PLACED = 4096
FLOPS = 2 * K * H * S + 2 * H * S * U + 2 * H * S * V


def tile_picked_ysmap_log_p_kernel(
    tc, x_words, x_scales, w1, e_words, e_scales, gain, offs, pos, neg, out
):
    nc = tc.nc
    with ExitStack() as ctx:
        keep = ctx.enter_context(tc.tile_pool(name="keep", bufs=1))
        placed = ctx.enter_context(tc.tile_pool(name="placed", bufs=1))
        psum = ctx.enter_context(tc.psum_pool(name="psum", bufs=1))

        offs_sb = keep.tile([P, S // 16], U16, name="offs_sb")
        neg_sb = keep.tile([P, U // 16], U16, name="neg_sb")
        pos_sb = keep.tile([P, V // 16], U16, name="pos_sb")
        xs_all = keep.tile([P, T], U8, name="xs_all", align_bytes=64)
        es_all = keep.tile([P, W], U8, name="es_all", align_bytes=64)
        xw_all = keep.tile([P, T], I32, name="xw_all", align_bytes=64)
        ew_all = keep.tile([P, W], I32, name="ew_all", align_bytes=64)
        w_raw = [keep.tile([P, j1 - j0, 4 * (m1 - m0)], F32, name=f"w_raw{a}", tag=f"w_raw{a}", align_bytes=64) for a, (j0, j1, m0, m1) in enumerate(W_PIECES)]
        gain_sb = keep.tile([P, V], F32, name="gain_sb")
        xs = keep.tile([P, S], U8, name="xs", align_bytes=64)
        es = keep.tile([P, (D + 1) * V], U8, name="es", align_bytes=64)

        nc.vector.memset(xs_all[0:ROW0, :].bitcast(I32), 0)
        nc.vector.memset(es_all[0:ROW0, :].bitcast(I32), 0)
        nc.vector.memset(xs[:].bitcast(I32), 0)
        nc.vector.memset(es[:].bitcast(I32), 0)

        w_view = w1.rearrange("(p j) c -> p j c", j=4)

        def load_w(a):
            j0, j1, m0, m1 = W_PIECES[a]
            nc.sync.dma_start(w_raw[a][:], w_view[:, j0:j1, 4 * m0 : 4 * m1])

        nc.sync.dma_start(offs_sb[:], offs)
        nc.scalar.dma_start(xs_all[ROW0:P, :].bitcast(I32), x_scales[0].bitcast(I32))
        load_w(0)
        nc.sync.dma_start(neg_sb[:], neg)
        nc.sync.dma_start(es_all[ROW0:P, :].bitcast(I32), e_scales[0].bitcast(I32))
        load_w(1)
        nc.sync.dma_start(pos_sb[:], pos)
        nc.sync.dma_start(xw_all[:], x_words[0].rearrange("p n t -> p (n t)").bitcast(I32))
        load_w(2)

        def place_rows(plane, picked):
            for q in range(4):
                nc.sync.dma_start(plane[32 * q : 32 * q + 4, :].bitcast(I32), picked[ROW0 + 4 * q : ROW0 + 4 * q + 4, :].bitcast(I32))

        xs_picked = keep.tile([P, S], U8, name="xs_picked", align_bytes=64)
        es_dealt = placed.tile([P, (D + 1) * V], U8, name="es_dealt", offset=HALF_PLACED - 384, align_bytes=64)
        pw = keep.tile([P, V], U32, name="pw", align_bytes=64)
        nw = keep.tile([P, D, V], U32, name="nw", align_bytes=64)

        nc.vector.tensor_copy(xs_picked[:], xs_all[:].indirect(offs_sb[:]))
        nc.vector.tensor_copy(es_dealt[:, 0:U].rearrange("p (d v) -> p v d", d=D), es_all[:].indirect(neg_sb[:]))
        nc.vector.tensor_copy(es_dealt[:, U : U + V], es_all[:].indirect(pos_sb[:]))
        place_rows(xs, xs_picked)
        nc.sync.dma_start(ew_all[:], e_words[0].rearrange("p n t -> p (n t)").bitcast(I32))
        place_rows(es, es_dealt)
        nc.sync.dma_start(gain_sb[:], gain)

        w_bf = keep.tile([P, 4, P, 4], BF16, name="w_bf", align_bytes=64)
        for a, (j0, j1, m0, m1) in enumerate(W_PIECES):
            for t0, t1 in ([(0, 2), (2, 4)] if a == len(W_PIECES) - 1 else [(0, 4)]):
                nc.scalar.activation(
                    w_bf[:, t0:t1, m0:m1, j0:j1].rearrange("p t m j -> p m j t"),
                    w_raw[a][:].rearrange("p j (m t) -> p m j t", t=4)[:, :, :, t0:t1],
                    ACT.Copy,
                )

        def gather_x_words(t0, t1, tag):
            picked = keep.tile([P, P * (t1 - t0)], U32, name=f"xw{t0}", tag=tag, align_bytes=64)
            nc.vector.tensor_copy(picked[:], xw_all[:].bitcast(U32).indirect(offs_sb[:, 8 * t0 : 8 * t1]))
            return [picked[:, P * i : P * (i + 1)] for i in range(t1 - t0)]

        xw = gather_x_words(0, X_EARLY, "xw0")
        wq = keep.tile([P, H], U32, name="wq", align_bytes=64)
        wq_s = keep.tile([P, H], U8, name="wq_s", align_bytes=64)
        for t in range(4):
            cols = slice(P * t, P * (t + 1))
            nc.vector.quantize_mx(out=wq[:, cols].bitcast(FP8X4), scales=wq_s[:, cols], in_=w_bf[:, t, :, :].rearrange("p m j -> p (m j)"))


        xw.extend(gather_x_words(X_EARLY, TILES, "w_raw2"))

        h_bf = []
        minus_all = placed.tile([P, TILES * 4 * P], BF16, name="minus_all", offset=0, align_bytes=64)
        codes_all = placed.tile([P, 2 * TILES * P], U32, name="codes_all", offset=HALF_PLACED, align_bytes=64)
        minus_h = [minus_all[:, 4 * P * i : 4 * P * (i + 1)] for i in range(TILES)]
        for i in range(TILES):
            h_ps = psum.tile([P, 4, P], F32, name="h_ps", tag="bank", bufs=8)
            for t in range(4):
                nc.tensor.matmul_mx(
                    out=h_ps[:, t, :],
                    lhsT=wq[:, P * t : P * (t + 1)].bitcast(FP8X4),
                    lhsT_scale=wq_s[:, P * t : P * (t + 1)],
                    rhs=xw[i].bitcast(FP8X4),
                    rhs_scale=xs[:, P * i : P * (i + 1)],
                    start=True,
                    stop=True,
                )
            h_bf.append(keep.tile([P, P, 4], BF16, name=f"h_bf{i}", align_bytes=64))
            nc.scalar.activation(h_bf[i][:], h_ps[:].rearrange("p t n -> p n t"), ACT.Copy)
            if i < SCALAR_NEGATES:
                nc.scalar.activation(minus_h[i].rearrange("p (n t) -> p n t", t=4), h_ps[:].rearrange("p t n -> p n t"), ACT.Copy, scale=-1.0)

        nc.vector.tensor_copy(pw[:], ew_all[:].bitcast(U32).indirect(pos_sb[:]))
        nc.vector.tensor_copy(nw[:].rearrange("p d v -> p v d"), ew_all[:].bitcast(U32).indirect(neg_sb[:]))

        def quantize(k, values):
            codes = codes_all[:, P * k : P * (k + 1)]
            scales = keep.tile([P, P], U8, name=f"h_scales{k}", align_bytes=64)
            nc.vector.quantize_mx(out=codes.bitcast(FP8X4), scales=scales[:], in_=values)
            return codes, scales

        th = keep.tile([P, TILES, D, V], F32, name="th")
        for i in range(TILES):
            if i >= SCALAR_NEGATES:
                nc.vector.tensor_scalar(minus_h[i], h_bf[i][:].rearrange("p n t -> p (n t)"), -1.0, None, ALU.mult)
            hq, hq_s = quantize(2 * i, h_bf[i][:].rearrange("p n t -> p (n t)"))
            mq, mq_s = quantize(2 * i + 1, minus_h[i])
            for members in [(0,), (1,)]:
                z_ps = psum.tile([P, D, V], F32, name="z_ps", tag="bank", bufs=8)
                for d in members:
                    nc.tensor.matmul_mx(out=z_ps[:, d, :], lhsT=hq.bitcast(FP8X4), lhsT_scale=hq_s[:],
                                        rhs=nw[:, d, :].bitcast(FP8X4), rhs_scale=es[:, V * d : V * (d + 1)], start=True, stop=False)
                    nc.tensor.matmul_mx(out=z_ps[:, d, :], lhsT=mq.bitcast(FP8X4), lhsT_scale=mq_s[:],
                                        rhs=pw[:].bitcast(FP8X4), rhs_scale=es[:, U : U + V], start=False, stop=True)
                ds = slice(members[0], members[-1] + 1)
                nc.scalar.activation(th[:, i, ds, :], z_ps[:, ds, :], ACT.Tanh, scale=2.0)

        sums = keep.tile([P, TILES, V], F32, name="sums")
        nc.vector.tensor_tensor(sums[:], th[:, :, 0, :], th[:, :, 1, :], ALU.add)

        HALF = V // 2
        for i in range(TILES):
            res = keep.tile([P, V], F32, name=f"res{i}")
            for c0, c1 in ([(0, HALF), (HALF, V)] if i in (0, TILES - 1) else [(0, V)]):
                lg = keep.tile([P, c1 - c0], F32, name=f"lg{i}_{c0}")
                nc.scalar.activation(lg[:], sums[:, i, c0:c1], ACT.Ln, scale=0.5, bias=2.0)
                nc.vector.tensor_tensor(res[:, c0:c1], lg[:], gain_sb[:, c0:c1], ALU.mult)
                if i == TILES - 1:
                    nc.sync.dma_start(out[P * i : P * (i + 1), c0:c1], res[:, c0:c1])
            if i < TILES - 1:
                nc.sync.dma_start(out[P * i : P * (i + 1), :], res[:])
